import numpy as np
import ml_dtypes


def mxq(x, axis, fmt="e4m3"):
    dtype, down = {"e4m3": (ml_dtypes.float8_e4m3fn, 7), "e5m2": (ml_dtypes.float8_e5m2, 14)}[fmt]
    v = np.moveaxis(np.asarray(x, np.float32).astype(ml_dtypes.bfloat16).astype(np.float64), axis, -1)
    blocks = v.reshape(v.shape[:-1] + (-1, 32))
    amax = np.abs(blocks).max(-1, keepdims=True)
    byte = np.maximum(np.where(amax > 0, np.frexp(amax)[1] - 1 + 127, 0) - down, 1)
    scale = np.exp2(byte - 127.0)
    codes = (blocks / scale).astype(np.float32).astype(dtype).astype(np.float64)
    return np.moveaxis((codes * scale).reshape(v.shape), -1, axis)


WIDE = False


def mx_kscale(k):
    if not WIDE:
        return np.ones(k)
    levels = np.array([10, -10, 5, -5, 0])
    if k % 512:
        return np.exp2(np.random.permutation(np.resize(levels, k // 32))).repeat(32)
    a = np.empty((k // 512, 16))
    for p in range(k // 512):
        a[p, :8] = np.random.permutation(np.resize(levels, 8))
        for g in range(8):
            far = levels[np.abs(levels - a[p, g]) >= 10]
            a[p, g + 8] = far[np.random.randint(len(far))]
    return np.exp2(a.ravel()).repeat(32)


def f64(x):
    return np.asarray(x).astype(np.float64)


def striped(idx):
    return np.tile(idx.reshape(-1, 16).T, (8, 1)).astype(np.uint16)


def unstriped(offs):
    return offs[:16].T.reshape(-1).astype(np.int64)


E2M1 = np.array([0.0, 0.5, 1.0, 1.5, 2.0, 3.0, 4.0, 6.0, -0.0, -0.5, -1.0, -1.5, -2.0, -3.0, -4.0, -6.0])


def pack_weight(w, fmt):
    k, n = w.shape
    w = f64(np.asarray(w, np.float32).astype(ml_dtypes.bfloat16)).reshape(k // 32, 32, n)
    amax = np.abs(w).max(1)
    if fmt == "e4m3":
        byte = np.frexp(amax)[1] - 1 + 127 - 7
    else:
        mant, ex = np.frexp(amax / 6.0)
        byte = np.where(mant > 0.5, ex, ex - 1) + 127
    byte = np.clip(np.where(amax > 0, byte, 1), 1, 254)
    scaled = (w * np.exp2(127.0 - byte)[:, None, :]).reshape(k, n).astype(np.float32)
    by_word = np.ascontiguousarray(scaled.reshape(k // 512, 128, 4, n).transpose(0, 1, 3, 2))
    if fmt == "e4m3":
        words = by_word.astype(ml_dtypes.float8_e4m3fn).view(np.uint8)
    else:
        c = by_word.astype(ml_dtypes.float4_e2m1fn).view(np.uint8) & 0xF
        words = (c[..., 0::2] | (c[..., 1::2] << 4)).reshape(k // 512, 128, 2 * n)
    return np.ascontiguousarray(words), np.ascontiguousarray(byte.astype(np.uint8).reshape(k // 512, 16, n))


def unpack_weight(words, scales, fmt):
    g, _, n = scales.shape
    words = np.ascontiguousarray(words).reshape(g, 128, n, -1)
    if fmt == "e4m3":
        vals = words.view(ml_dtypes.float8_e4m3fn).astype(np.float64)
    else:
        nib = np.empty((g, 128, n, 4), np.uint8)
        nib[..., 0::2] = words & 0xF
        nib[..., 1::2] = words >> 4
        vals = E2M1[nib]
    vals = vals * np.repeat(np.exp2(scales.astype(np.float64) - 127.0), 8, axis=1)[..., None]
    return vals.transpose(0, 1, 3, 2).reshape(g * 512, n)


K, M, T, S = 1024, 1024, 4096, 2048


def setup_inputs():
    n = np.random.standard_normal
    s = mx_kscale(K)[:, None]
    u = mx_kscale(512)[:, None]
    v = pack_weight(n((K, T)) * s, "e4m3")
    p_w4 = pack_weight(n((K, M)) / np.sqrt(K) / s, "e2m1")
    return {
        "tab_words": v[0],
        "tab_scales": v[1],
        "w4_words": p_w4[0],
        "w4_scales": p_w4[1],
        "down": (n((K, 512)) / np.sqrt(K) / s * u.T).astype(np.float32),
        "up": (0.5 * n((512, M)) / np.sqrt(512) / u).astype(np.float32),
        "gT": n((M, T)).astype(np.float32),
        "b": (0.3 * n(1024)).astype(np.float32),
        "offs": striped(np.random.permutation(T)[:S]),
    }


def reference(tab_words, tab_scales, w4_words, w4_scales, down, up, gT, b, offs):
    tab_ = unpack_weight(tab_words, tab_scales, "e4m3")[:, unstriped(offs)]
    w4_ = unpack_weight(w4_words, w4_scales, "e2m1")
    down_ = mxq(f64(down), 0, "e4m3")
    up_ = mxq(f64(up), 0, "e4m3")
    h_ = mxq(down_.T @ tab_, 0, "e4m3")
    y = w4_.T @ tab_ + up_.T @ h_
    return (y + f64(b)[:, None]) * f64(gT)[:, unstriped(offs)]

@@ -1,0 +1,209 @@
+from contextlib import ExitStack
+
+import concourse.mybir as mybir
+from concourse.masks import make_identity
+
+K, M, T, S, R = 1024, 1024, 4096, 2048, 512
+FLOPS = 2 * S * (K * M + K * R + R * M)
+
+F32 = mybir.dt.float32
+BF16 = mybir.dt.bfloat16
+I32 = mybir.dt.int32
+U32 = mybir.dt.uint32
+U16 = mybir.dt.uint16
+U8 = mybir.dt.uint8
+FP8X4 = mybir.dt.float8_e4m3fn_x4
+FP4X4 = mybir.dt.float4_e2m1fn_x4
+MULT = mybir.AluOpType.mult
+IDENTITY = mybir.ActivationFunctionType.Identity
+
+P = 128
+PACK = 4
+PASSES = K // (P * PACK)
+CHUNK = 512
+CHUNKS = S // CHUNK
+BLOCK = 128
+ROW_TILES = M // P
+LIST_ROWS = 16
+UP_PART = 256
+GATE = 1024
+
+
+def tile_list_tabgate_bias_kernel(
+    tc, tab_words, tab_scales, w4_words, w4_scales, down, up, gT, b, offs, out
+):
+    nc = tc.nc
+    with ExitStack() as ctx:
+        keep = ctx.enter_context(tc.tile_pool(name="keep", bufs=1))
+        big = ctx.enter_context(tc.tile_pool(name="big", bufs=8))
+        stage = ctx.enter_context(tc.tile_pool(name="stage", bufs=4))
+        ypool = ctx.enter_context(tc.tile_pool(name="ypool", bufs=4))
+        psum_h = ctx.enter_context(tc.psum_pool(name="psum_h", bufs=3))
+        psum_y = ctx.enter_context(tc.psum_pool(name="psum_y", bufs=4))
+        psum_b = ctx.enter_context(tc.psum_pool(name="psum_b", bufs=1))
+
+        offsets = keep.tile([P, S // LIST_ROWS], U16, name="offsets")
+        nc.sync.dma_start(offsets[:], offs)
+
+        def entries(j0, j1):
+            return offsets[:, j0 // LIST_ROWS : j1 // LIST_ROWS]
+
+        tab_sc = keep.tile([P, PASSES, T // 4], I32, name="tab_sc", align_bytes=64)
+        w4_sc = keep.tile([P, PASSES, M // 4], I32, name="w4_sc", align_bytes=64)
+        nc.vector.memset(tab_sc[:], 0)
+        nc.vector.memset(w4_sc[:], 0)
+        for src, dst in ((tab_scales, tab_sc), (w4_scales, w4_sc)):
+            for q in range(4):
+                nc.gpsimd.dma_start(
+                    dst[32 * q : 32 * q + 4, :, :],
+                    src[:, 4 * q : 4 * q + 4, :].rearrange("a r t -> r a t").bitcast(I32),
+                )
+
+        b_rows = keep.tile([P, P], F32, name="b_rows")
+        ident = keep.tile([P, P], F32, name="ident")
+        bias = keep.tile([P, ROW_TILES], F32, name="bias")
+        nc.vector.memset(b_rows[:], 0.0)
+        nc.gpsimd.dma_start(b_rows[0:ROW_TILES, :], b.rearrange("(m p) -> m p", p=P))
+        make_identity(nc, ident[:])
+        b_psum = psum_b.tile([P, P], F32, name="b_psum")
+        nc.tensor.transpose(b_psum[:], b_rows[:], ident[:])
+        nc.scalar.copy(bias[:], b_psum[:, 0:ROW_TILES])
+
+        def load_words(a):
+            words = big.tile([P, T], I32, name="words", tag="big", align_bytes=64)
+            nc.sync.dma_start(words[:], tab_words[a].rearrange("p t i -> p (t i)").bitcast(I32))
+            return words
+
+        words0 = load_words(0)
+        down_raw = big.tile([P, PASSES, PACK, R], F32, name="down_raw", tag="big", align_bytes=64)
+        for a in range(PASSES):
+            nc.sync.dma_start(
+                down_raw[:, a, :, :],
+                down[a * P * PACK : (a + 1) * P * PACK, :].rearrange("(p i) r -> p i r", i=PACK),
+            )
+        words1 = load_words(1)
+        up_raw = big.tile([P, PACK, M], F32, name="up_raw", tag="big", align_bytes=64)
+        nc.sync.dma_start(up_raw[:], up.rearrange("(p i) n -> p i n", i=PACK))
+        w4 = keep.tile([P, PASSES, 2 * M // 4], I32, name="w4", align_bytes=64)
+        nc.sync.dma_start(w4[:], w4_words.rearrange("a p c -> p a c").bitcast(I32))
+        gates = []
+        for m in range(ROW_TILES):
+            gate = big.tile([P, T], F32, name="gate", tag="big", align_bytes=64)
+            nc.sync.dma_start(gate[:], gT[m * P : (m + 1) * P, :])
+            gates.append(gate)
+
+        v_codes = keep.tile([P, PASSES, S], U32, name="v_codes", align_bytes=64)
+        v_sc = keep.tile([P, PASSES, S], U8, name="v_sc", align_bytes=64)
+        down_codes = keep.tile([P, PASSES, R], U32, name="down_codes", align_bytes=64)
+        down_sc = keep.tile([P, PASSES, R], U8, name="down_sc", align_bytes=64)
+        up_codes = keep.tile([P, M], U32, name="up_codes", align_bytes=64)
+        up_sc = keep.tile([P, M], U8, name="up_sc", align_bytes=64)
+        h_codes = keep.tile([P, S], U32, name="h_codes", align_bytes=64)
+        h_sc = keep.tile([P, S], U8, name="h_sc", align_bytes=64)
+
+        def gather_words(words, a, j0, j1):
+            nc.vector.tensor_copy(v_codes[:, a, j0:j1], words[:].bitcast(U32).indirect(entries(j0, j1)))
+
+        def gather_scales(a, j0, j1):
+            nc.vector.tensor_copy(v_sc[:, a, j0:j1], tab_sc[:, a, :].bitcast(U8).indirect(entries(j0, j1)))
+
+        def quantize_down(a):
+            grouped = stage.tile([P, PACK * R], BF16, name="grouped", tag="stage", align_bytes=64)
+            nc.scalar.copy(
+                grouped[:].rearrange("p (t m i) -> p m t i", t=PACK, i=PACK),
+                down_raw[:, a, :, :].rearrange("p i (m t) -> p m t i", t=PACK),
+            )
+            nc.vector.quantize_mx(down_codes[:, a, :].bitcast(FP8X4), down_sc[:, a, :], grouped[:])
+
+        def quantize_up(part):
+            cols = slice(part * UP_PART, (part + 1) * UP_PART)
+            grouped = stage.tile([P, PACK * UP_PART], BF16, name="grouped", tag="stage", align_bytes=64)
+            nc.scalar.copy(
+                grouped[:].rearrange("p (n i) -> p n i", i=PACK),
+                up_raw[:, :, cols].rearrange("p i n -> p n i"),
+            )
+            nc.vector.quantize_mx(up_codes[:, cols].bitcast(FP8X4), up_sc[:, cols], grouped[:])
+
+        def make_h(c):
+            grouped = stage.tile([P, PACK * CHUNK], BF16, name="grouped", tag="stage", align_bytes=64)
+            for blk in range(CHUNK // BLOCK):
+                j0 = c * CHUNK + blk * BLOCK
+                bank = psum_h.tile([P, PACK, BLOCK], F32, name="h_bank")
+                for t in range(PACK):
+                    for a in range(PASSES):
+                        nc.tensor.matmul_mx(
+                            bank[:, t, :],
+                            lhsT=down_codes[:, a, t * P : (t + 1) * P].bitcast(FP8X4),
+                            lhsT_scale=down_sc[:, a, t * P : (t + 1) * P],
+                            rhs=v_codes[:, a, j0 : j0 + BLOCK].bitcast(FP8X4),
+                            rhs_scale=v_sc[:, a, j0 : j0 + BLOCK],
+                            start=(a == 0),
+                            stop=(a == PASSES - 1),
+                        )
+                nc.scalar.copy(
+                    grouped[:, PACK * BLOCK * blk : PACK * BLOCK * (blk + 1)].rearrange("p (n t) -> p n t", t=PACK),
+                    bank[:].rearrange("p t n -> p n t"),
+                )
+            cols = slice(c * CHUNK, (c + 1) * CHUNK)
+            nc.vector.quantize_mx(h_codes[:, cols].bitcast(FP8X4), h_sc[:, cols], grouped[:])
+
+        gather_words(words0, 0, 0, S)
+        for half in range(2):
+            j0, j1 = half * S // 2, (half + 1) * S // 2
+            for a in range(PASSES):
+                gather_scales(a, j0, j1)
+            if half == 0:
+                for a in range(PASSES):
+                    quantize_down(a)
+            chunks = range(half * CHUNKS // 2, (half + 1) * CHUNKS // 2)
+            for c in chunks:
+                gather_words(words1, 1, c * CHUNK, (c + 1) * CHUNK)
+            for c in chunks:
+                make_h(c)
+            if half == 0:
+                quantize_up(0)
+
+        for m in range(ROW_TILES):
+            rows = slice(m * P, (m + 1) * P)
+            if m == 0:
+                pair = keep.tile([P, 2, S], F32, name="first_pair", align_bytes=64)
+            elif m % 2 == 0:
+                pair = big.tile([P, 2, S], F32, name="pair", tag="big", align_bytes=64)
+            result = pair[:, m % 2, :]
+            for g in range(S // GATE):
+                y = ypool.tile([P, GATE], F32, name="y")
+                for u in range(GATE // CHUNK):
+                    j0 = g * GATE + u * CHUNK
+                    cols = slice(j0, j0 + CHUNK)
+                    bank = psum_y.tile([P, CHUNK], F32, name="y_bank")
+                    for a in range(PASSES):
+                        nc.tensor.matmul_mx(
+                            bank[:],
+                            lhsT=w4[:, a, :].bitcast(U8)[:, 2 * m * P : 2 * (m + 1) * P].bitcast(FP4X4),
+                            lhsT_scale=w4_sc[:, a, :].bitcast(U8)[:, rows],
+                            rhs=v_codes[:, a, cols].bitcast(FP8X4),
+                            rhs_scale=v_sc[:, a, cols],
+                            start=(a == 0),
+                            stop=False,
+                        )
+                    nc.tensor.matmul_mx(
+                        bank[:],
+                        lhsT=up_codes[:, rows].bitcast(FP8X4),
+                        lhsT_scale=up_sc[:, rows],
+                        rhs=h_codes[:, cols].bitcast(FP8X4),
+                        rhs_scale=h_sc[:, cols],
+                        start=False,
+                        stop=True,
+                    )
+                    nc.scalar.activation(
+                        y[:, u * CHUNK : (u + 1) * CHUNK], bank[:], IDENTITY, bias=bias[:, m : m + 1]
+                    )
+                nc.vector.tensor_tensor(
+                    result[:, g * GATE : (g + 1) * GATE],
+                    gates[m][:].indirect(entries(g * GATE, (g + 1) * GATE)),
+                    y[:],
+                    MULT,
+                )
+            nc.sync.dma_start(out[rows, :], result)
+            if m % 2 == 0 and m // 2 + 1 < M // UP_PART:
+                quantize_up(m // 2 + 1)

@@ -50,11 +50,12 @@ def tile_list_tabgate_bias_kernel(
 
         tab_sc = keep.tile([P, PASSES, T // 4], I32, name="tab_sc", align_bytes=64)
         w4_sc = keep.tile([P, PASSES, M // 4], I32, name="w4_sc", align_bytes=64)
-        nc.vector.memset(tab_sc[:], 0)
-        nc.vector.memset(w4_sc[:], 0)
+        nc.vector.memset(tab_sc[:, 0, :], 0)
+        nc.gpsimd.memset(tab_sc[:, 1, :], 0)
+        nc.gpsimd.memset(w4_sc[:], 0)
         for src, dst in ((tab_scales, tab_sc), (w4_scales, w4_sc)):
             for q in range(4):
-                nc.gpsimd.dma_start(
+                nc.sync.dma_start(
                     dst[32 * q : 32 * q + 4, :, :],
                     src[:, 4 * q : 4 * q + 4, :].rearrange("a r t -> r a t").bitcast(I32),
                 )
@@ -62,30 +63,36 @@ def tile_list_tabgate_bias_kernel(
         b_rows = keep.tile([P, P], F32, name="b_rows")
         ident = keep.tile([P, P], F32, name="ident")
         bias = keep.tile([P, ROW_TILES], F32, name="bias")
-        nc.vector.memset(b_rows[:], 0.0)
-        nc.gpsimd.dma_start(b_rows[0:ROW_TILES, :], b.rearrange("(m p) -> m p", p=P))
+        nc.gpsimd.memset(b_rows[:], 0.0)
+        nc.sync.dma_start(b_rows[0:ROW_TILES, :], b.rearrange("(m p) -> m p", p=P))
         make_identity(nc, ident[:])
         b_psum = psum_b.tile([P, P], F32, name="b_psum")
         nc.tensor.transpose(b_psum[:], b_rows[:], ident[:])
         nc.scalar.copy(bias[:], b_psum[:, 0:ROW_TILES])
 
         def load_words(a):
-            words = big.tile([P, T], I32, name="words", tag="big", align_bytes=64)
-            nc.sync.dma_start(words[:], tab_words[a].rearrange("p t i -> p (t i)").bitcast(I32))
-            return words
+            window = big.tile([P, T], I32, name="window", tag="big", align_bytes=64)
+            nc.sync.dma_start(window[:], tab_words[a].rearrange("p t i -> p (t i)").bitcast(I32))
+            return window
 
-        words0 = load_words(0)
+        up_raw = big.tile([P, PACK, M], F32, name="up_raw", tag="big", align_bytes=64)
+        up_rows = up.rearrange("(p i) n -> p i n", i=PACK)
+
+        def load_up(n0, n1):
+            nc.sync.dma_start(up_raw[:, :, n0:n1], up_rows[:, :, n0:n1])
+
+        load_up(0, UP_PART)
         down_raw = big.tile([P, PASSES, PACK, R], F32, name="down_raw", tag="big", align_bytes=64)
         for a in range(PASSES):
             nc.sync.dma_start(
                 down_raw[:, a, :, :],
                 down[a * P * PACK : (a + 1) * P * PACK, :].rearrange("(p i) r -> p i r", i=PACK),
             )
-        words1 = load_words(1)
-        up_raw = big.tile([P, PACK, M], F32, name="up_raw", tag="big", align_bytes=64)
-        nc.sync.dma_start(up_raw[:], up.rearrange("(p i) n -> p i n", i=PACK))
+        load_up(UP_PART, 2 * UP_PART)
+        words = [load_words(a) for a in range(PASSES)]
         w4 = keep.tile([P, PASSES, 2 * M // 4], I32, name="w4", align_bytes=64)
         nc.sync.dma_start(w4[:], w4_words.rearrange("a p c -> p a c").bitcast(I32))
+        load_up(2 * UP_PART, M)
         gates = []
         for m in range(ROW_TILES):
             gate = big.tile([P, T], F32, name="gate", tag="big", align_bytes=64)
@@ -101,8 +108,8 @@ def tile_list_tabgate_bias_kernel(
         h_codes = keep.tile([P, S], U32, name="h_codes", align_bytes=64)
         h_sc = keep.tile([P, S], U8, name="h_sc", align_bytes=64)
 
-        def gather_words(words, a, j0, j1):
-            nc.vector.tensor_copy(v_codes[:, a, j0:j1], words[:].bitcast(U32).indirect(entries(j0, j1)))
+        def gather_words(a, j0, j1):
+            nc.vector.tensor_copy(v_codes[:, a, j0:j1], words[a][:].bitcast(U32).indirect(entries(j0, j1)))
 
         def gather_scales(a, j0, j1):
             nc.vector.tensor_copy(v_sc[:, a, j0:j1], tab_sc[:, a, :].bitcast(U8).indirect(entries(j0, j1)))
@@ -147,21 +154,19 @@ def tile_list_tabgate_bias_kernel(
             cols = slice(c * CHUNK, (c + 1) * CHUNK)
             nc.vector.quantize_mx(h_codes[:, cols].bitcast(FP8X4), h_sc[:, cols], grouped[:])
 
-        gather_words(words0, 0, 0, S)
+        for a in range(PASSES):
+            gather_scales(a, 0, S)
+        for a in range(PASSES):
+            quantize_down(a)
+        for part in range(2):
+            quantize_up(part)
         for half in range(2):
-            j0, j1 = half * S // 2, (half + 1) * S // 2
-            for a in range(PASSES):
-                gather_scales(a, j0, j1)
-            if half == 0:
-                for a in range(PASSES):
-                    quantize_down(a)
+            gather_words(0, half * S // 2, (half + 1) * S // 2)
             chunks = range(half * CHUNKS // 2, (half + 1) * CHUNKS // 2)
             for c in chunks:
-                gather_words(words1, 1, c * CHUNK, (c + 1) * CHUNK)
+                gather_words(1, c * CHUNK, (c + 1) * CHUNK)
             for c in chunks:
                 make_h(c)
-            if half == 0:
-                quantize_up(0)
 
         for m in range(ROW_TILES):
             rows = slice(m * P, (m + 1) * P)
@@ -204,6 +209,9 @@ def tile_list_tabgate_bias_kernel(
                     y[:],
                     MULT,
                 )
-            nc.sync.dma_start(out[rows, :], result)
-            if m % 2 == 0 and m // 2 + 1 < M // UP_PART:
-                quantize_up(m // 2 + 1)
+                if m == ROW_TILES - 1:
+                    nc.sync.dma_start(out[rows, g * GATE : (g + 1) * GATE], result[:, g * GATE : (g + 1) * GATE])
+            if m < ROW_TILES - 1:
+                nc.sync.dma_start(out[rows, :], result)
+            if m < 2:
+                quantize_up(2 + m)

@@ -27,6 +27,7 @@ ROW_TILES = M // P
 LIST_ROWS = 16
 UP_PART = 256
 GATE = 1024
+BIG_SLOTS = 6
 
 
 def tile_list_tabgate_bias_kernel(
@@ -35,8 +36,9 @@ def tile_list_tabgate_bias_kernel(
     nc = tc.nc
     with ExitStack() as ctx:
         keep = ctx.enter_context(tc.tile_pool(name="keep", bufs=1))
-        big = ctx.enter_context(tc.tile_pool(name="big", bufs=8))
-        stage = ctx.enter_context(tc.tile_pool(name="stage", bufs=4))
+        big = ctx.enter_context(tc.tile_pool(name="big", bufs=BIG_SLOTS))
+        results = ctx.enter_context(tc.tile_pool(name="results", bufs=2))
+        stage = ctx.enter_context(tc.tile_pool(name="stage", bufs=6))
         ypool = ctx.enter_context(tc.tile_pool(name="ypool", bufs=4))
         psum_h = ctx.enter_context(tc.psum_pool(name="psum_h", bufs=3))
         psum_y = ctx.enter_context(tc.psum_pool(name="psum_y", bufs=4))
@@ -48,17 +50,13 @@ def tile_list_tabgate_bias_kernel(
         def entries(j0, j1):
             return offsets[:, j0 // LIST_ROWS : j1 // LIST_ROWS]
 
-        tab_sc = keep.tile([P, PASSES, T // 4], I32, name="tab_sc", align_bytes=64)
-        w4_sc = keep.tile([P, PASSES, M // 4], I32, name="w4_sc", align_bytes=64)
-        nc.vector.memset(tab_sc[:, 0, :], 0)
-        nc.gpsimd.memset(tab_sc[:, 1, :], 0)
-        nc.gpsimd.memset(w4_sc[:], 0)
-        for src, dst in ((tab_scales, tab_sc), (w4_scales, w4_sc)):
-            for q in range(4):
-                nc.sync.dma_start(
-                    dst[32 * q : 32 * q + 4, :, :],
-                    src[:, 4 * q : 4 * q + 4, :].rearrange("a r t -> r a t").bitcast(I32),
-                )
+        tab_sc = big.tile([P, T // 4], I32, name="tab_sc", tag="big")
+        nc.vector.memset(tab_sc[:, : T // 8], 0)
+        nc.gpsimd.memset(tab_sc[:, T // 8 :], 0)
+        for q in (0, 2, 1, 3):
+            nc.sync.dma_start(
+                tab_sc[32 * q : 32 * q + 4 * PASSES, :], tab_scales[:, 4 * q : 4 * q + 4, :].bitcast(I32)
+            )
 
         b_rows = keep.tile([P, P], F32, name="b_rows")
         ident = keep.tile([P, P], F32, name="ident")
@@ -71,36 +69,43 @@ def tile_list_tabgate_bias_kernel(
         nc.scalar.copy(bias[:], b_psum[:, 0:ROW_TILES])
 
         def load_words(a):
-            window = big.tile([P, T], I32, name="window", tag="big", align_bytes=64)
+            window = big.tile([P, T], I32, name="window", tag="big")
             nc.sync.dma_start(window[:], tab_words[a].rearrange("p t i -> p (t i)").bitcast(I32))
             return window
 
-        up_raw = big.tile([P, PACK, M], F32, name="up_raw", tag="big", align_bytes=64)
-        up_rows = up.rearrange("(p i) n -> p i n", i=PACK)
-
-        def load_up(n0, n1):
-            nc.sync.dma_start(up_raw[:, :, n0:n1], up_rows[:, :, n0:n1])
-
-        load_up(0, UP_PART)
-        down_raw = big.tile([P, PASSES, PACK, R], F32, name="down_raw", tag="big", align_bytes=64)
-        for a in range(PASSES):
-            nc.sync.dma_start(
-                down_raw[:, a, :, :],
-                down[a * P * PACK : (a + 1) * P * PACK, :].rearrange("(p i) r -> p i r", i=PACK),
-            )
-        load_up(UP_PART, 2 * UP_PART)
+        down_raw = big.tile([P, PASSES, PACK, R], F32, name="down_raw", tag="big")
+        down_rows = down.rearrange("(a p i) r -> a p i r", p=P, i=PACK)
+        for i in range(0, PACK, 2):
+            nc.sync.dma_start(down_raw[:, 0, i : i + 2, :], down_rows[0, :, i : i + 2, :])
+        nc.sync.dma_start(down_raw[:, 1, :, :], down_rows[1])
         words = [load_words(a) for a in range(PASSES)]
+        w4_sc = keep.tile([P, PASSES, M // 4], I32, name="w4_sc", align_bytes=64)
+        nc.gpsimd.memset(w4_sc[:], 0)
+        for r in range(4):
+            nc.sync.dma_start(
+                w4_sc[r:P:32, :, :], w4_scales[:, r:16:4, :].rearrange("a q n -> q a n").bitcast(I32)
+            )
+        up_raw = big.tile([P, PACK, M], F32, name="up_raw", tag="big")
+        up_rows = up.rearrange("(p i) n -> p i n", i=PACK)
+        nc.sync.dma_start(up_raw[:, :, :UP_PART], up_rows[:, :, :UP_PART])
         w4 = keep.tile([P, PASSES, 2 * M // 4], I32, name="w4", align_bytes=64)
         nc.sync.dma_start(w4[:], w4_words.rearrange("a p c -> p a c").bitcast(I32))
-        load_up(2 * UP_PART, M)
+        nc.sync.dma_start(up_raw[:, :, UP_PART:], up_rows[:, :, UP_PART:])
+
+        v_sc = keep.tile([P, S], U8, name="v_sc", align_bytes=64)
+        nc.vector.tensor_copy(v_sc[:], tab_sc[:].bitcast(U8).indirect(offsets[:]))
+        v_sc1 = keep.tile([P, S // 4], I32, name="v_sc1", align_bytes=64)
+        nc.gpsimd.memset(v_sc1[:], 0)
+        for r in range(4):
+            nc.sync.dma_start(v_sc1[r:P:32, :], v_sc[4 + r : P : 32, :].bitcast(I32))
+
         gates = []
         for m in range(ROW_TILES):
-            gate = big.tile([P, T], F32, name="gate", tag="big", align_bytes=64)
+            gate = big.tile([P, T], F32, name="gate", tag="big")
             nc.sync.dma_start(gate[:], gT[m * P : (m + 1) * P, :])
             gates.append(gate)
 
         v_codes = keep.tile([P, PASSES, S], U32, name="v_codes", align_bytes=64)
-        v_sc = keep.tile([P, PASSES, S], U8, name="v_sc", align_bytes=64)
         down_codes = keep.tile([P, PASSES, R], U32, name="down_codes", align_bytes=64)
         down_sc = keep.tile([P, PASSES, R], U8, name="down_sc", align_bytes=64)
         up_codes = keep.tile([P, M], U32, name="up_codes", align_bytes=64)
@@ -110,9 +115,6 @@ def tile_list_tabgate_bias_kernel(
 
         def gather_words(a, j0, j1):
             nc.vector.tensor_copy(v_codes[:, a, j0:j1], words[a][:].bitcast(U32).indirect(entries(j0, j1)))
-
-        def gather_scales(a, j0, j1):
-            nc.vector.tensor_copy(v_sc[:, a, j0:j1], tab_sc[:, a, :].bitcast(U8).indirect(entries(j0, j1)))
 
         def quantize_down(a):
             grouped = stage.tile([P, PACK * R], BF16, name="grouped", tag="stage", align_bytes=64)
@@ -143,7 +145,7 @@ def tile_list_tabgate_bias_kernel(
                             lhsT=down_codes[:, a, t * P : (t + 1) * P].bitcast(FP8X4),
                             lhsT_scale=down_sc[:, a, t * P : (t + 1) * P],
                             rhs=v_codes[:, a, j0 : j0 + BLOCK].bitcast(FP8X4),
-                            rhs_scale=v_sc[:, a, j0 : j0 + BLOCK],
+                            rhs_scale=v_sc[4 * a :, j0 : j0 + BLOCK],
                             start=(a == 0),
                             stop=(a == PASSES - 1),
                         )
@@ -155,25 +157,24 @@ def tile_list_tabgate_bias_kernel(
             nc.vector.quantize_mx(h_codes[:, cols].bitcast(FP8X4), h_sc[:, cols], grouped[:])
 
         for a in range(PASSES):
-            gather_scales(a, 0, S)
-        for a in range(PASSES):
             quantize_down(a)
-        for part in range(2):
-            quantize_up(part)
         for half in range(2):
             gather_words(0, half * S // 2, (half + 1) * S // 2)
             chunks = range(half * CHUNKS // 2, (half + 1) * CHUNKS // 2)
             for c in chunks:
                 gather_words(1, c * CHUNK, (c + 1) * CHUNK)
+            if half == 0:
+                quantize_up(0)
             for c in chunks:
                 make_h(c)
 
         for m in range(ROW_TILES):
             rows = slice(m * P, (m + 1) * P)
-            if m == 0:
-                pair = keep.tile([P, 2, S], F32, name="first_pair", align_bytes=64)
-            elif m % 2 == 0:
-                pair = big.tile([P, 2, S], F32, name="pair", tag="big", align_bytes=64)
+            if m % 2 == 0:
+                if m < ROW_TILES // 2:
+                    pair = results.tile([P, 2, S], F32, name="pair")
+                else:
+                    pair = big.tile([P, 2, S], F32, name="pair", tag="big")
             result = pair[:, m % 2, :]
             for g in range(S // GATE):
                 y = ypool.tile([P, GATE], F32, name="y")
@@ -187,7 +188,7 @@ def tile_list_tabgate_bias_kernel(
                             lhsT=w4[:, a, :].bitcast(U8)[:, 2 * m * P : 2 * (m + 1) * P].bitcast(FP4X4),
                             lhsT_scale=w4_sc[:, a, :].bitcast(U8)[:, rows],
                             rhs=v_codes[:, a, cols].bitcast(FP8X4),
-                            rhs_scale=v_sc[:, a, cols],
+                            rhs_scale=(v_sc[:] if a == 0 else v_sc1[:].bitcast(U8))[:, cols],
                             start=(a == 0),
                             stop=False,
                         )
@@ -209,9 +210,10 @@ def tile_list_tabgate_bias_kernel(
                     y[:],
                     MULT,
                 )
+                step = m * (S // GATE) + g
+                if step + 1 < M // UP_PART:
+                    quantize_up(step + 1)
                 if m == ROW_TILES - 1:
                     nc.sync.dma_start(out[rows, g * GATE : (g + 1) * GATE], result[:, g * GATE : (g + 1) * GATE])
             if m < ROW_TILES - 1:
                 nc.sync.dma_start(out[rows, :], result)
-            if m < 2:
-                quantize_up(2 + m)

@@ -26,7 +26,6 @@ BLOCK = 128
 ROW_TILES = M // P
 LIST_ROWS = 16
 UP_PART = 256
-GATE = 1024
 BIG_SLOTS = 6
 
 
@@ -176,12 +175,22 @@ def tile_list_tabgate_bias_kernel(
                 else:
                     pair = big.tile([P, 2, S], F32, name="pair", tag="big")
             result = pair[:, m % 2, :]
-            for g in range(S // GATE):
-                y = ypool.tile([P, GATE], F32, name="y")
-                for u in range(GATE // CHUNK):
-                    j0 = g * GATE + u * CHUNK
-                    cols = slice(j0, j0 + CHUNK)
+            edges = (0, 2 * CHUNK, 3 * CHUNK, S) if m == ROW_TILES - 1 else (0, 2 * CHUNK, S)
+            for g, (j_start, j_end) in enumerate(zip(edges, edges[1:])):
+                span = slice(j_start, j_end)
+                y = ypool.tile([P, j_end - j_start], F32, name="y")
+                for u in range((j_end - j_start) // CHUNK):
+                    cols = slice(j_start + u * CHUNK, j_start + (u + 1) * CHUNK)
                     bank = psum_y.tile([P, CHUNK], F32, name="y_bank")
+                    nc.tensor.matmul_mx(
+                        bank[:],
+                        lhsT=up_codes[:, rows].bitcast(FP8X4),
+                        lhsT_scale=up_sc[:, rows],
+                        rhs=h_codes[:, cols].bitcast(FP8X4),
+                        rhs_scale=h_sc[:, cols],
+                        start=True,
+                        stop=False,
+                    )
                     for a in range(PASSES):
                         nc.tensor.matmul_mx(
                             bank[:],
@@ -189,31 +198,19 @@ def tile_list_tabgate_bias_kernel(
                             lhsT_scale=w4_sc[:, a, :].bitcast(U8)[:, rows],
                             rhs=v_codes[:, a, cols].bitcast(FP8X4),
                             rhs_scale=(v_sc[:] if a == 0 else v_sc1[:].bitcast(U8))[:, cols],
-                            start=(a == 0),
-                            stop=False,
+                            start=False,
+                            stop=(a == PASSES - 1),
                         )
-                    nc.tensor.matmul_mx(
-                        bank[:],
-                        lhsT=up_codes[:, rows].bitcast(FP8X4),
-                        lhsT_scale=up_sc[:, rows],
-                        rhs=h_codes[:, cols].bitcast(FP8X4),
-                        rhs_scale=h_sc[:, cols],
-                        start=False,
-                        stop=True,
-                    )
                     nc.scalar.activation(
                         y[:, u * CHUNK : (u + 1) * CHUNK], bank[:], IDENTITY, bias=bias[:, m : m + 1]
                     )
                 nc.vector.tensor_tensor(
-                    result[:, g * GATE : (g + 1) * GATE],
-                    gates[m][:].indirect(entries(g * GATE, (g + 1) * GATE)),
-                    y[:],
-                    MULT,
+                    result[:, span], gates[m][:].indirect(entries(j_start, j_end)), y[:], MULT
                 )
-                step = m * (S // GATE) + g
-                if step + 1 < M // UP_PART:
-                    quantize_up(step + 1)
+                part = 2 * m + g + 1
+                if part < M // UP_PART:
+                    quantize_up(part)
                 if m == ROW_TILES - 1:
-                    nc.sync.dma_start(out[rows, g * GATE : (g + 1) * GATE], result[:, g * GATE : (g + 1) * GATE])
+                    nc.sync.dma_start(out[rows, span], result[:, span])
             if m < ROW_TILES - 1:
                 nc.sync.dma_start(out[rows, :], result)

@@ -26,7 +26,15 @@ BLOCK = 128
 ROW_TILES = M // P
 LIST_ROWS = 16
 UP_PART = 256
-BIG_SLOTS = 6
+GATE_AT = (0, 16, 48, 89, 65, 105, 121, 137)
+WORDS_AT = (32, 65)
+DOWN_AT = (48, 57)
+BIAS_AT = 64
+V1_AT = 81
+UP_CODES_AT = (169, 171, 173, 174)
+UP_GROUPED_AT = (85, 32, 169, 171)
+H_GROUPED_AT = (87, 119, 137, 141)
+RESULT_AT = (153, 161, 0, 8, 16, 24, 48, 56)
 
 
 def tile_list_tabgate_bias_kernel(
@@ -35,13 +43,13 @@ def tile_list_tabgate_bias_kernel(
     nc = tc.nc
     with ExitStack() as ctx:
         keep = ctx.enter_context(tc.tile_pool(name="keep", bufs=1))
-        big = ctx.enter_context(tc.tile_pool(name="big", bufs=BIG_SLOTS))
-        results = ctx.enter_context(tc.tile_pool(name="results", bufs=2))
-        stage = ctx.enter_context(tc.tile_pool(name="stage", bufs=6))
+        space = ctx.enter_context(tc.tile_pool(name="space", bufs=1))
         ypool = ctx.enter_context(tc.tile_pool(name="ypool", bufs=4))
-        psum_h = ctx.enter_context(tc.psum_pool(name="psum_h", bufs=3))
+        psum_h = ctx.enter_context(tc.psum_pool(name="psum_h", bufs=4))
         psum_y = ctx.enter_context(tc.psum_pool(name="psum_y", bufs=4))
-        psum_b = ctx.enter_context(tc.psum_pool(name="psum_b", bufs=1))
+
+        def placed(shape, dtype, name, kib):
+            return space.tile(shape, dtype, name=name, offset=kib * 1024, align_bytes=64)
 
         offsets = keep.tile([P, S // LIST_ROWS], U16, name="offsets")
         nc.sync.dma_start(offsets[:], offs)
@@ -49,47 +57,48 @@ def tile_list_tabgate_bias_kernel(
         def entries(j0, j1):
             return offsets[:, j0 // LIST_ROWS : j1 // LIST_ROWS]
 
-        tab_sc = big.tile([P, T // 4], I32, name="tab_sc", tag="big")
-        nc.vector.memset(tab_sc[:, : T // 8], 0)
-        nc.gpsimd.memset(tab_sc[:, T // 8 :], 0)
+        tab_sc = placed([P, T // 4], I32, "tab_sc", GATE_AT[0])
+        nc.vector.memset(tab_sc[:], 0)
         for q in (0, 2, 1, 3):
             nc.sync.dma_start(
                 tab_sc[32 * q : 32 * q + 4 * PASSES, :], tab_scales[:, 4 * q : 4 * q + 4, :].bitcast(I32)
             )
 
-        b_rows = keep.tile([P, P], F32, name="b_rows")
+        def load_words(a, edges):
+            window = placed([P, T], I32, "window%d" % a, WORDS_AT[a])
+            rows = tab_words[a].rearrange("p t i -> p (t i)").bitcast(I32)
+            for t0, t1 in zip(edges, edges[1:]):
+                nc.sync.dma_start(window[:, t0:t1], rows[:, t0:t1])
+            return window
+
+        def load_down(a):
+            raw = placed([P, PACK, R], F32, "down_raw%d" % a, DOWN_AT[a])
+            nc.sync.dma_start(raw[:], down.rearrange("(a p i) r -> a p i r", p=P, i=PACK)[a])
+            return raw
+
+        words = [load_words(0, (0, T // 8, T // 4, T))]
+        down_raw = [load_down(a) for a in range(PASSES)]
+
+        b_rows = placed([P, P], F32, "b_rows", GATE_AT[1])
         ident = keep.tile([P, P], F32, name="ident")
-        bias = keep.tile([P, ROW_TILES], F32, name="bias")
         nc.gpsimd.memset(b_rows[:], 0.0)
         nc.sync.dma_start(b_rows[0:ROW_TILES, :], b.rearrange("(m p) -> m p", p=P))
         make_identity(nc, ident[:])
-        b_psum = psum_b.tile([P, P], F32, name="b_psum")
+        b_psum = psum_h.tile([P, P], F32, name="b_psum", tag="h_bank")
         nc.tensor.transpose(b_psum[:], b_rows[:], ident[:])
-        nc.scalar.copy(bias[:], b_psum[:, 0:ROW_TILES])
 
-        def load_words(a):
-            window = big.tile([P, T], I32, name="window", tag="big")
-            nc.sync.dma_start(window[:], tab_words[a].rearrange("p t i -> p (t i)").bitcast(I32))
-            return window
-
-        down_raw = big.tile([P, PASSES, PACK, R], F32, name="down_raw", tag="big")
-        down_rows = down.rearrange("(a p i) r -> a p i r", p=P, i=PACK)
-        for i in range(0, PACK, 2):
-            nc.sync.dma_start(down_raw[:, 0, i : i + 2, :], down_rows[0, :, i : i + 2, :])
-        nc.sync.dma_start(down_raw[:, 1, :, :], down_rows[1])
-        words = [load_words(a) for a in range(PASSES)]
         w4_sc = keep.tile([P, PASSES, M // 4], I32, name="w4_sc", align_bytes=64)
         nc.gpsimd.memset(w4_sc[:], 0)
         for r in range(4):
             nc.sync.dma_start(
                 w4_sc[r:P:32, :, :], w4_scales[:, r:16:4, :].rearrange("a q n -> q a n").bitcast(I32)
             )
-        up_raw = big.tile([P, PACK, M], F32, name="up_raw", tag="big")
+        words.append(load_words(1, (0, T)))
         up_rows = up.rearrange("(p i) n -> p i n", i=PACK)
-        nc.sync.dma_start(up_raw[:, :, :UP_PART], up_rows[:, :, :UP_PART])
+        up_first = placed([P, PACK, UP_PART], F32, "up_first", GATE_AT[3])
+        nc.sync.dma_start(up_first[:], up_rows[:, :, :UP_PART])
         w4 = keep.tile([P, PASSES, 2 * M // 4], I32, name="w4", align_bytes=64)
         nc.sync.dma_start(w4[:], w4_words.rearrange("a p c -> p a c").bitcast(I32))
-        nc.sync.dma_start(up_raw[:, :, UP_PART:], up_rows[:, :, UP_PART:])
 
         v_sc = keep.tile([P, S], U8, name="v_sc", align_bytes=64)
         nc.vector.tensor_copy(v_sc[:], tab_sc[:].bitcast(U8).indirect(offsets[:]))
@@ -99,54 +108,65 @@ def tile_list_tabgate_bias_kernel(
             nc.sync.dma_start(v_sc1[r:P:32, :], v_sc[4 + r : P : 32, :].bitcast(I32))
 
         gates = []
-        for m in range(ROW_TILES):
-            gate = big.tile([P, T], F32, name="gate", tag="big")
+
+        def load_gate(m):
+            gate = placed([P, T], F32, "gate%d" % m, GATE_AT[m])
             nc.sync.dma_start(gate[:], gT[m * P : (m + 1) * P, :])
             gates.append(gate)
 
-        v_codes = keep.tile([P, PASSES, S], U32, name="v_codes", align_bytes=64)
-        down_codes = keep.tile([P, PASSES, R], U32, name="down_codes", align_bytes=64)
+        load_gate(0)
+
+        v_codes0 = keep.tile([P, S], U32, name="v_codes0", align_bytes=64)
+        v_codes1 = [placed([P, CHUNK], U32, "v_codes1_%d" % c, V1_AT + 2 * c) for c in range(CHUNKS)]
+        down_codes = placed([P, PASSES, R], U32, "down_codes", WORDS_AT[0])
         down_sc = keep.tile([P, PASSES, R], U8, name="down_sc", align_bytes=64)
-        up_codes = keep.tile([P, M], U32, name="up_codes", align_bytes=64)
+        up_codes = [placed([P, UP_PART], U32, "up_codes%d" % part, UP_CODES_AT[part]) for part in range(M // UP_PART)]
         up_sc = keep.tile([P, M], U8, name="up_sc", align_bytes=64)
         h_codes = keep.tile([P, S], U32, name="h_codes", align_bytes=64)
         h_sc = keep.tile([P, S], U8, name="h_sc", align_bytes=64)
 
+        def v_codes(a, j0, j1):
+            if a == 0:
+                return v_codes0[:, j0:j1]
+            c = j0 // CHUNK
+            return v_codes1[c][:, j0 - c * CHUNK : j1 - c * CHUNK]
+
         def gather_words(a, j0, j1):
-            nc.vector.tensor_copy(v_codes[:, a, j0:j1], words[a][:].bitcast(U32).indirect(entries(j0, j1)))
+            nc.vector.tensor_copy(v_codes(a, j0, j1), words[a][:].bitcast(U32).indirect(entries(j0, j1)))
 
         def quantize_down(a):
-            grouped = stage.tile([P, PACK * R], BF16, name="grouped", tag="stage", align_bytes=64)
+            grouped = placed([P, PACK * R], BF16, "down_grouped%d" % a, V1_AT + 4 * (1 - a))
             nc.scalar.copy(
-                grouped[:].rearrange("p (t m i) -> p m t i", t=PACK, i=PACK),
-                down_raw[:, a, :, :].rearrange("p i (m t) -> p m t i", t=PACK),
+                grouped[:].rearrange("p (t m i) -> p m i t", t=PACK, i=PACK),
+                down_raw[a][:].rearrange("p i (m t) -> p m i t", t=PACK),
             )
             nc.vector.quantize_mx(down_codes[:, a, :].bitcast(FP8X4), down_sc[:, a, :], grouped[:])
 
         def quantize_up(part):
             cols = slice(part * UP_PART, (part + 1) * UP_PART)
-            grouped = stage.tile([P, PACK * UP_PART], BF16, name="grouped", tag="stage", align_bytes=64)
+            raw = up_first[:] if part == 0 else up_rest[:, :, cols.start - UP_PART : cols.stop - UP_PART]
+            grouped = placed([P, PACK * UP_PART], BF16, "up_grouped%d" % part, UP_GROUPED_AT[part])[:]
             nc.scalar.copy(
-                grouped[:].rearrange("p (n i) -> p n i", i=PACK),
-                up_raw[:, :, cols].rearrange("p i n -> p n i"),
+                grouped.rearrange("p (c n i) -> p c i n", n=PACK, i=PACK),
+                raw.rearrange("p i (c n) -> p c i n", n=PACK),
             )
-            nc.vector.quantize_mx(up_codes[:, cols].bitcast(FP8X4), up_sc[:, cols], grouped[:])
+            nc.vector.quantize_mx(up_codes[part][:].bitcast(FP8X4), up_sc[:, cols], grouped)
 
         def make_h(c):
-            grouped = stage.tile([P, PACK * CHUNK], BF16, name="grouped", tag="stage", align_bytes=64)
+            grouped = placed([P, PACK * CHUNK], BF16, "h_grouped%d" % c, H_GROUPED_AT[c])
             for blk in range(CHUNK // BLOCK):
                 j0 = c * CHUNK + blk * BLOCK
-                bank = psum_h.tile([P, PACK, BLOCK], F32, name="h_bank")
-                for t in range(PACK):
-                    for a in range(PASSES):
+                bank = psum_h.tile([P, PACK, BLOCK], F32, name="h_bank", tag="h_bank")
+                for a in range(PASSES):
+                    for t in range(PACK):
                         nc.tensor.matmul_mx(
                             bank[:, t, :],
                             lhsT=down_codes[:, a, t * P : (t + 1) * P].bitcast(FP8X4),
                             lhsT_scale=down_sc[:, a, t * P : (t + 1) * P],
-                            rhs=v_codes[:, a, j0 : j0 + BLOCK].bitcast(FP8X4),
+                            rhs=v_codes(a, j0, j0 + BLOCK).bitcast(FP8X4),
                             rhs_scale=v_sc[4 * a :, j0 : j0 + BLOCK],
-                            start=(a == 0),
-                            stop=(a == PASSES - 1),
+                            start=(a == 0 and t == 0),
+                            stop=(a == PASSES - 1 and t == PACK - 1),
                         )
                 nc.scalar.copy(
                     grouped[:, PACK * BLOCK * blk : PACK * BLOCK * (blk + 1)].rearrange("p (n t) -> p n t", t=PACK),
@@ -155,62 +175,79 @@ def tile_list_tabgate_bias_kernel(
             cols = slice(c * CHUNK, (c + 1) * CHUNK)
             nc.vector.quantize_mx(h_codes[:, cols].bitcast(FP8X4), h_sc[:, cols], grouped[:])
 
-        for a in range(PASSES):
-            quantize_down(a)
-        for half in range(2):
-            gather_words(0, half * S // 2, (half + 1) * S // 2)
-            chunks = range(half * CHUNKS // 2, (half + 1) * CHUNKS // 2)
-            for c in chunks:
-                gather_words(1, c * CHUNK, (c + 1) * CHUNK)
-            if half == 0:
-                quantize_up(0)
-            for c in chunks:
-                make_h(c)
-
-        for m in range(ROW_TILES):
+        def gated(m, result, j_start, j_end):
             rows = slice(m * P, (m + 1) * P)
-            if m % 2 == 0:
-                if m < ROW_TILES // 2:
-                    pair = results.tile([P, 2, S], F32, name="pair")
-                else:
-                    pair = big.tile([P, 2, S], F32, name="pair", tag="big")
-            result = pair[:, m % 2, :]
-            edges = (0, 2 * CHUNK, 3 * CHUNK, S) if m == ROW_TILES - 1 else (0, 2 * CHUNK, S)
-            for g, (j_start, j_end) in enumerate(zip(edges, edges[1:])):
-                span = slice(j_start, j_end)
-                y = ypool.tile([P, j_end - j_start], F32, name="y")
-                for u in range((j_end - j_start) // CHUNK):
-                    cols = slice(j_start + u * CHUNK, j_start + (u + 1) * CHUNK)
-                    bank = psum_y.tile([P, CHUNK], F32, name="y_bank")
+            y = ypool.tile([P, j_end - j_start], F32, name="y")
+            for u in range((j_end - j_start) // CHUNK):
+                cols = slice(j_start + u * CHUNK, j_start + (u + 1) * CHUNK)
+                bank = psum_y.tile([P, CHUNK], F32, name="y_bank")
+                nc.tensor.matmul_mx(
+                    bank[:],
+                    lhsT=up_codes[m // 2][:, (m % 2) * P : (m % 2 + 1) * P].bitcast(FP8X4),
+                    lhsT_scale=up_sc[:, rows],
+                    rhs=h_codes[:, cols].bitcast(FP8X4),
+                    rhs_scale=h_sc[:, cols],
+                    start=True,
+                    stop=False,
+                )
+                for a in range(PASSES):
                     nc.tensor.matmul_mx(
                         bank[:],
-                        lhsT=up_codes[:, rows].bitcast(FP8X4),
-                        lhsT_scale=up_sc[:, rows],
-                        rhs=h_codes[:, cols].bitcast(FP8X4),
-                        rhs_scale=h_sc[:, cols],
-                        start=True,
-                        stop=False,
+                        lhsT=w4[:, a, :].bitcast(U8)[:, 2 * m * P : 2 * (m + 1) * P].bitcast(FP4X4),
+                        lhsT_scale=w4_sc[:, a, :].bitcast(U8)[:, rows],
+                        rhs=v_codes(a, cols.start, cols.stop).bitcast(FP8X4),
+                        rhs_scale=(v_sc[:] if a == 0 else v_sc1[:].bitcast(U8))[:, cols],
+                        start=False,
+                        stop=(a == PASSES - 1),
                     )
-                    for a in range(PASSES):
-                        nc.tensor.matmul_mx(
-                            bank[:],
-                            lhsT=w4[:, a, :].bitcast(U8)[:, 2 * m * P : 2 * (m + 1) * P].bitcast(FP4X4),
-                            lhsT_scale=w4_sc[:, a, :].bitcast(U8)[:, rows],
-                            rhs=v_codes[:, a, cols].bitcast(FP8X4),
-                            rhs_scale=(v_sc[:] if a == 0 else v_sc1[:].bitcast(U8))[:, cols],
-                            start=False,
-                            stop=(a == PASSES - 1),
-                        )
-                    nc.scalar.activation(
-                        y[:, u * CHUNK : (u + 1) * CHUNK], bank[:], IDENTITY, bias=bias[:, m : m + 1]
-                    )
-                nc.vector.tensor_tensor(
-                    result[:, span], gates[m][:].indirect(entries(j_start, j_end)), y[:], MULT
-                )
-                part = 2 * m + g + 1
-                if part < M // UP_PART:
-                    quantize_up(part)
-                if m == ROW_TILES - 1:
-                    nc.sync.dma_start(out[rows, span], result[:, span])
-            if m < ROW_TILES - 1:
-                nc.sync.dma_start(out[rows, :], result)
+                nc.scalar.activation(y[:, u * CHUNK : (u + 1) * CHUNK], bank[:], IDENTITY, bias=bias[:, m : m + 1])
+            nc.vector.tensor_tensor(
+                result[:, j_start:j_end], gates[m][:].indirect(entries(j_start, j_end)), y[:], MULT
+            )
+
+        def result_tile(m):
+            return placed([P, S], F32, "result%d" % m, RESULT_AT[m])
+
+        gather_words(0, 0, S)
+        up_rest = placed([P, PACK, M - UP_PART], F32, "up_rest", WORDS_AT[0] + 4)
+        nc.sync.dma_start(up_rest[:], up_rows[:, :, UP_PART:])
+        for a in range(PASSES):
+            quantize_down(a)
+        bias = placed([P, ROW_TILES], F32, "bias", BIAS_AT)
+        nc.scalar.copy(bias[:], b_psum[:, 0:ROW_TILES])
+        load_gate(1)
+        load_gate(2)
+        gather_words(1, 0, CHUNK)
+        gather_words(1, CHUNK, 2 * CHUNK)
+        quantize_up(0)
+        gather_words(1, 2 * CHUNK, 3 * CHUNK)
+        make_h(0)
+        load_gate(3)
+        gather_words(1, 3 * CHUNK, 4 * CHUNK)
+        load_gate(4)
+        make_h(1)
+        load_gate(5)
+        load_gate(6)
+        result = result_tile(0)
+        for c in range(CHUNKS):
+            gated(0, result, c * CHUNK, (c + 1) * CHUNK)
+            if c + 2 < CHUNKS:
+                make_h(c + 2)
+            if c == 1:
+                quantize_up(1)
+        load_gate(7)
+        nc.sync.dma_start(out[0:P, :], result[:])
+
+        for m in range(1, ROW_TILES):
+            rows = slice(m * P, (m + 1) * P)
+            result = result_tile(m)
+            last = m == ROW_TILES - 1
+            edges = (0, 2 * CHUNK, 3 * CHUNK, S) if last else (0, 2 * CHUNK, S)
+            for j_start, j_end in zip(edges, edges[1:]):
+                gated(m, result, j_start, j_end)
+                if last:
+                    nc.sync.dma_start(out[rows, j_start:j_end], result[:, j_start:j_end])
+            if m in (1, 3):
+                quantize_up((m + 3) // 2)
+            if not last:
+                nc.sync.dma_start(out[rows, :], result[:])

@@ -26,15 +26,19 @@ BLOCK = 128
 ROW_TILES = M // P
 LIST_ROWS = 16
 UP_PART = 256
-GATE_AT = (0, 16, 48, 89, 65, 105, 121, 137)
-WORDS_AT = (32, 65)
-DOWN_AT = (48, 57)
-BIAS_AT = 64
-V1_AT = 81
-UP_CODES_AT = (169, 171, 173, 174)
-UP_GROUPED_AT = (85, 32, 169, 171)
-H_GROUPED_AT = (87, 119, 137, 141)
-RESULT_AT = (153, 161, 0, 8, 16, 24, 48, 56)
+GATE_AT = (52, 68, 92, 0, 108, 124, 140, 156)
+WORDS_AT = (37, 0)
+TAB_SC_AT = 15
+UP_AT = 18
+W4_AT = 34
+DOWN_CODES_AT = 39
+DOWN_AT = (68, 76)
+V1_AT = 84
+UP_CODES_AT = (43, 45, 47, 48)
+DOWN_SC_AT = 49
+UP_GROUPED_AT = (172, 49, 43, 45)
+H_GROUPED_AT = (90, 108, 124, 154)
+RESULT_AT = (172, 180, 52, 60, 68, 76, 92, 100)
 
 
 def tile_list_tabgate_bias_kernel(
@@ -57,55 +61,20 @@ def tile_list_tabgate_bias_kernel(
         def entries(j0, j1):
             return offsets[:, j0 // LIST_ROWS : j1 // LIST_ROWS]
 
-        tab_sc = placed([P, T // 4], I32, "tab_sc", GATE_AT[0])
-        nc.vector.memset(tab_sc[:], 0)
-        for q in (0, 2, 1, 3):
-            nc.sync.dma_start(
-                tab_sc[32 * q : 32 * q + 4 * PASSES, :], tab_scales[:, 4 * q : 4 * q + 4, :].bitcast(I32)
-            )
+        tab_sc = placed([P, T // 4], I32, "tab_sc", TAB_SC_AT)
+        nc.sync.dma_start(tab_sc[0:32, :], tab_scales.rearrange("a q t -> (a q) t").bitcast(I32))
+        nc.vector.memset(tab_sc[64:128, :], 0)
+        nc.vector.memset(tab_sc[32:64, :], 0)
 
-        def load_words(a, edges):
+        def load_words(a):
             window = placed([P, T], I32, "window%d" % a, WORDS_AT[a])
-            rows = tab_words[a].rearrange("p t i -> p (t i)").bitcast(I32)
-            for t0, t1 in zip(edges, edges[1:]):
-                nc.sync.dma_start(window[:, t0:t1], rows[:, t0:t1])
+            nc.sync.dma_start(window[:], tab_words[a].rearrange("p t i -> p (t i)").bitcast(I32))
             return window
 
         def load_down(a):
             raw = placed([P, PACK, R], F32, "down_raw%d" % a, DOWN_AT[a])
             nc.sync.dma_start(raw[:], down.rearrange("(a p i) r -> a p i r", p=P, i=PACK)[a])
             return raw
-
-        words = [load_words(0, (0, T // 8, T // 4, T))]
-        down_raw = [load_down(a) for a in range(PASSES)]
-
-        b_rows = placed([P, P], F32, "b_rows", GATE_AT[1])
-        ident = keep.tile([P, P], F32, name="ident")
-        nc.gpsimd.memset(b_rows[:], 0.0)
-        nc.sync.dma_start(b_rows[0:ROW_TILES, :], b.rearrange("(m p) -> m p", p=P))
-        make_identity(nc, ident[:])
-        b_psum = psum_h.tile([P, P], F32, name="b_psum", tag="h_bank")
-        nc.tensor.transpose(b_psum[:], b_rows[:], ident[:])
-
-        w4_sc = keep.tile([P, PASSES, M // 4], I32, name="w4_sc", align_bytes=64)
-        nc.gpsimd.memset(w4_sc[:], 0)
-        for r in range(4):
-            nc.sync.dma_start(
-                w4_sc[r:P:32, :, :], w4_scales[:, r:16:4, :].rearrange("a q n -> q a n").bitcast(I32)
-            )
-        words.append(load_words(1, (0, T)))
-        up_rows = up.rearrange("(p i) n -> p i n", i=PACK)
-        up_first = placed([P, PACK, UP_PART], F32, "up_first", GATE_AT[3])
-        nc.sync.dma_start(up_first[:], up_rows[:, :, :UP_PART])
-        w4 = keep.tile([P, PASSES, 2 * M // 4], I32, name="w4", align_bytes=64)
-        nc.sync.dma_start(w4[:], w4_words.rearrange("a p c -> p a c").bitcast(I32))
-
-        v_sc = keep.tile([P, S], U8, name="v_sc", align_bytes=64)
-        nc.vector.tensor_copy(v_sc[:], tab_sc[:].bitcast(U8).indirect(offsets[:]))
-        v_sc1 = keep.tile([P, S // 4], I32, name="v_sc1", align_bytes=64)
-        nc.gpsimd.memset(v_sc1[:], 0)
-        for r in range(4):
-            nc.sync.dma_start(v_sc1[r:P:32, :], v_sc[4 + r : P : 32, :].bitcast(I32))
 
         gates = []
 
@@ -114,12 +83,41 @@ def tile_list_tabgate_bias_kernel(
             nc.sync.dma_start(gate[:], gT[m * P : (m + 1) * P, :])
             gates.append(gate)
 
-        load_gate(0)
+        words = [load_words(0)]
+        down_raw = [load_down(a) for a in range(PASSES)]
+
+        picked_sc = keep.tile([P, S], U8, name="picked_sc", align_bytes=64)
+        nc.vector.tensor_copy(picked_sc[:], tab_sc[:].bitcast(U8).indirect(offsets[:]))
+        v_sc = []
+
+        def place_scales(a):
+            plane = keep.tile([P, S // 4], I32, name="v_sc%d" % a, align_bytes=64)
+            nc.gpsimd.memset(plane[:], 0)
+            for r in range(4):
+                nc.sync.dma_start(plane[r:P:32, :], picked_sc[16 * a + r : 16 * (a + 1) : 4, :].bitcast(I32))
+            v_sc.append(plane[:].bitcast(U8))
+
+        place_scales(0)
+        words.append(load_words(1))
+        place_scales(1)
+        up_raw = placed([P, PACK, M], F32, "up_raw", UP_AT)
+        nc.sync.dma_start(up_raw[:], up.rearrange("(p i) n -> p i n", i=PACK))
+        w4_sc = keep.tile([P, PASSES, M // 4], I32, name="w4_sc", align_bytes=64)
+        nc.gpsimd.memset(w4_sc[:], 0)
+        for r in range(4):
+            nc.gpsimd.dma_start(
+                w4_sc[r:P:32, :, :], w4_scales[:, r:16:4, :].rearrange("a q n -> q a n").bitcast(I32)
+            )
+        b_rows = keep.tile([P, P], F32, name="b_rows")
+        ident = keep.tile([P, P], F32, name="ident")
+        nc.gpsimd.memset(b_rows[:], 0.0)
+        nc.gpsimd.dma_start(b_rows[0:ROW_TILES, :], b.rearrange("(m p) -> m p", p=P))
+        make_identity(nc, ident[:])
 
         v_codes0 = keep.tile([P, S], U32, name="v_codes0", align_bytes=64)
         v_codes1 = [placed([P, CHUNK], U32, "v_codes1_%d" % c, V1_AT + 2 * c) for c in range(CHUNKS)]
-        down_codes = placed([P, PASSES, R], U32, "down_codes", WORDS_AT[0])
-        down_sc = keep.tile([P, PASSES, R], U8, name="down_sc", align_bytes=64)
+        down_codes = placed([P, PASSES, R], U32, "down_codes", DOWN_CODES_AT)
+        down_sc = placed([P, PASSES, R], U8, "down_sc", DOWN_SC_AT)
         up_codes = [placed([P, UP_PART], U32, "up_codes%d" % part, UP_CODES_AT[part]) for part in range(M // UP_PART)]
         up_sc = keep.tile([P, M], U8, name="up_sc", align_bytes=64)
         h_codes = keep.tile([P, S], U32, name="h_codes", align_bytes=64)
@@ -144,7 +142,7 @@ def tile_list_tabgate_bias_kernel(
 
         def quantize_up(part):
             cols = slice(part * UP_PART, (part + 1) * UP_PART)
-            raw = up_first[:] if part == 0 else up_rest[:, :, cols.start - UP_PART : cols.stop - UP_PART]
+            raw = up_raw[:, :, cols]
             grouped = placed([P, PACK * UP_PART], BF16, "up_grouped%d" % part, UP_GROUPED_AT[part])[:]
             nc.scalar.copy(
                 grouped.rearrange("p (c n i) -> p c i n", n=PACK, i=PACK),
@@ -164,7 +162,7 @@ def tile_list_tabgate_bias_kernel(
                             lhsT=down_codes[:, a, t * P : (t + 1) * P].bitcast(FP8X4),
                             lhsT_scale=down_sc[:, a, t * P : (t + 1) * P],
                             rhs=v_codes(a, j0, j0 + BLOCK).bitcast(FP8X4),
-                            rhs_scale=v_sc[4 * a :, j0 : j0 + BLOCK],
+                            rhs_scale=v_sc[a][:, j0 : j0 + BLOCK],
                             start=(a == 0 and t == 0),
                             stop=(a == PASSES - 1 and t == PACK - 1),
                         )
@@ -180,7 +178,7 @@ def tile_list_tabgate_bias_kernel(
             y = ypool.tile([P, j_end - j_start], F32, name="y")
             for u in range((j_end - j_start) // CHUNK):
                 cols = slice(j_start + u * CHUNK, j_start + (u + 1) * CHUNK)
-                bank = psum_y.tile([P, CHUNK], F32, name="y_bank")
+                bank = psum_y.tile([P, CHUNK], F32, name="y_bank", tag="y_bank")
                 nc.tensor.matmul_mx(
                     bank[:],
                     lhsT=up_codes[m // 2][:, (m % 2) * P : (m % 2 + 1) * P].bitcast(FP8X4),
@@ -196,7 +194,7 @@ def tile_list_tabgate_bias_kernel(
                         lhsT=w4[:, a, :].bitcast(U8)[:, 2 * m * P : 2 * (m + 1) * P].bitcast(FP4X4),
                         lhsT_scale=w4_sc[:, a, :].bitcast(U8)[:, rows],
                         rhs=v_codes(a, cols.start, cols.stop).bitcast(FP8X4),
-                        rhs_scale=(v_sc[:] if a == 0 else v_sc1[:].bitcast(U8))[:, cols],
+                        rhs_scale=v_sc[a][:, cols],
                         start=False,
                         stop=(a == PASSES - 1),
                     )
@@ -209,45 +207,41 @@ def tile_list_tabgate_bias_kernel(
             return placed([P, S], F32, "result%d" % m, RESULT_AT[m])
 
         gather_words(0, 0, S)
-        up_rest = placed([P, PACK, M - UP_PART], F32, "up_rest", WORDS_AT[0] + 4)
-        nc.sync.dma_start(up_rest[:], up_rows[:, :, UP_PART:])
+        w4 = placed([P, PASSES, 2 * M // 4], I32, "w4", W4_AT)
+        nc.sync.dma_start(w4[:], w4_words.rearrange("a p c -> p a c").bitcast(I32))
+        load_gate(0)
         for a in range(PASSES):
             quantize_down(a)
-        bias = placed([P, ROW_TILES], F32, "bias", BIAS_AT)
-        nc.scalar.copy(bias[:], b_psum[:, 0:ROW_TILES])
         load_gate(1)
-        load_gate(2)
-        gather_words(1, 0, CHUNK)
-        gather_words(1, CHUNK, 2 * CHUNK)
-        quantize_up(0)
-        gather_words(1, 2 * CHUNK, 3 * CHUNK)
+        for c in range(CHUNKS - 1):
+            gather_words(1, c * CHUNK, (c + 1) * CHUNK)
         make_h(0)
+        load_gate(2)
+        gather_words(1, S - CHUNK, S)
         load_gate(3)
-        gather_words(1, 3 * CHUNK, 4 * CHUNK)
-        load_gate(4)
+        quantize_up(0)
+        b_psum = psum_y.tile([P, P], F32, name="b_psum", tag="y_bank")
+        nc.tensor.transpose(b_psum[:], b_rows[:], ident[:])
+        bias = keep.tile([P, ROW_TILES], F32, name="bias")
+        nc.scalar.copy(bias[:], b_psum[:, 0:ROW_TILES])
         make_h(1)
-        load_gate(5)
-        load_gate(6)
+        load_gate(4)
         result = result_tile(0)
         for c in range(CHUNKS):
             gated(0, result, c * CHUNK, (c + 1) * CHUNK)
             if c + 2 < CHUNKS:
                 make_h(c + 2)
+                load_gate(c + 5)
             if c == 1:
+                load_gate(7)
                 quantize_up(1)
-        load_gate(7)
         nc.sync.dma_start(out[0:P, :], result[:])
 
         for m in range(1, ROW_TILES):
             rows = slice(m * P, (m + 1) * P)
             result = result_tile(m)
-            last = m == ROW_TILES - 1
-            edges = (0, 2 * CHUNK, 3 * CHUNK, S) if last else (0, 2 * CHUNK, S)
-            for j_start, j_end in zip(edges, edges[1:]):
-                gated(m, result, j_start, j_end)
-                if last:
-                    nc.sync.dma_start(out[rows, j_start:j_end], result[:, j_start:j_end])
+            for half in range(2):
+                gated(m, result, half * S // 2, (half + 1) * S // 2)
             if m in (1, 3):
                 quantize_up((m + 3) // 2)
-            if not last:
-                nc.sync.dma_start(out[rows, :], result[:])
+            nc.sync.dma_start(out[rows, :], result[:])

@@ -240,8 +240,13 @@ def tile_list_tabgate_bias_kernel(
         for m in range(1, ROW_TILES):
             rows = slice(m * P, (m + 1) * P)
             result = result_tile(m)
-            for half in range(2):
-                gated(m, result, half * S // 2, (half + 1) * S // 2)
+            last = m == ROW_TILES - 1
+            edges = (0, 2 * CHUNK, 3 * CHUNK, S) if last else (0, 2 * CHUNK, S)
+            for j_start, j_end in zip(edges, edges[1:]):
+                gated(m, result, j_start, j_end)
+                if last:
+                    nc.sync.dma_start(out[rows, j_start:j_end], result[:, j_start:j_end])
             if m in (1, 3):
                 quantize_up((m + 3) // 2)
-            nc.sync.dma_start(out[rows, :], result[:])
+            if not last:
+                nc.sync.dma_start(out[rows, :], result[:])

@@ -31,13 +31,18 @@ WORDS_AT = (37, 0)
 TAB_SC_AT = 15
 UP_AT = 18
 W4_AT = 34
-DOWN_CODES_AT = 39
+DOWN_CODES_AT = 180
+W4_SC_AT = 16
 DOWN_AT = (68, 76)
 V1_AT = 84
-UP_CODES_AT = (43, 45, 47, 48)
-DOWN_SC_AT = 49
-UP_GROUPED_AT = (172, 49, 43, 45)
-H_GROUPED_AT = (90, 108, 124, 154)
+V0_LAST_AT = 194
+DOWN_GROUPED_AT = (V0_LAST_AT, V1_AT)
+UP_CODES_AT = (43, 60, 76, 100)
+B_ROW = 24
+DOWN_SC_AT = 184
+UP_GROUPED_AT = (172, 188, 190, 192)
+H_GROUPED_AT = (92, 108, 124, 154)
+H_BLOCKS_ON_VECTOR = (8, 9, 10, 13)
 RESULT_AT = (172, 180, 52, 60, 68, 76, 92, 100)
 
 
@@ -49,8 +54,7 @@ def tile_list_tabgate_bias_kernel(
         keep = ctx.enter_context(tc.tile_pool(name="keep", bufs=1))
         space = ctx.enter_context(tc.tile_pool(name="space", bufs=1))
         ypool = ctx.enter_context(tc.tile_pool(name="ypool", bufs=4))
-        psum_h = ctx.enter_context(tc.psum_pool(name="psum_h", bufs=4))
-        psum_y = ctx.enter_context(tc.psum_pool(name="psum_y", bufs=4))
+        psum = ctx.enter_context(tc.psum_pool(name="psum", bufs=8))
 
         def placed(shape, dtype, name, kib):
             return space.tile(shape, dtype, name=name, offset=kib * 1024, align_bytes=64)
@@ -63,6 +67,24 @@ def tile_list_tabgate_bias_kernel(
 
         tab_sc = placed([P, T // 4], I32, "tab_sc", TAB_SC_AT)
         nc.sync.dma_start(tab_sc[0:32, :], tab_scales.rearrange("a q t -> (a q) t").bitcast(I32))
+        b_rows = keep.tile([P, P], F32, name="b_rows")
+        ident = keep.tile([P, P], F32, name="ident")
+        nc.sync.dma_start(b_rows[B_ROW : B_ROW + ROW_TILES, :], b.rearrange("(m p) -> m p", p=P))
+        nc.gpsimd.memset(b_rows[0:B_ROW, :], 0.0)
+        nc.gpsimd.memset(b_rows[32:64, :], 0.0)
+        nc.gpsimd.memset(b_rows[64:128, :], 0.0)
+        make_identity(nc, ident[:])
+        b_psum = psum.tile([P, P], F32, name="b_psum", tag="bank")
+        nc.tensor.transpose(b_psum[:], b_rows[:], ident[:])
+        early = len(UP_GROUPED_AT) - 1
+        bias = []
+        for m in range(early):
+            column = placed([P, 1], F32, "bias%d" % m, UP_GROUPED_AT[m + 1])
+            nc.scalar.copy(column[:], b_psum[:, B_ROW + m : B_ROW + m + 1])
+            bias.append(column[:])
+        late_bias = keep.tile([P, ROW_TILES - early], F32, name="late_bias")
+        nc.scalar.copy(late_bias[:], b_psum[:, B_ROW + early : B_ROW + ROW_TILES])
+        bias.extend(late_bias[:, m : m + 1] for m in range(ROW_TILES - early))
         nc.vector.memset(tab_sc[64:128, :], 0)
         nc.vector.memset(tab_sc[32:64, :], 0)
 
@@ -92,7 +114,7 @@ def tile_list_tabgate_bias_kernel(
 
         def place_scales(a):
             plane = keep.tile([P, S // 4], I32, name="v_sc%d" % a, align_bytes=64)
-            nc.gpsimd.memset(plane[:], 0)
+            nc.vector.memset(plane[:], 0)
             for r in range(4):
                 nc.sync.dma_start(plane[r:P:32, :], picked_sc[16 * a + r : 16 * (a + 1) : 4, :].bitcast(I32))
             v_sc.append(plane[:].bitcast(U8))
@@ -102,38 +124,32 @@ def tile_list_tabgate_bias_kernel(
         place_scales(1)
         up_raw = placed([P, PACK, M], F32, "up_raw", UP_AT)
         nc.sync.dma_start(up_raw[:], up.rearrange("(p i) n -> p i n", i=PACK))
-        w4_sc = keep.tile([P, PASSES, M // 4], I32, name="w4_sc", align_bytes=64)
-        nc.gpsimd.memset(w4_sc[:], 0)
+        w4_sc = placed([P, PASSES, M // 4], I32, "w4_sc", W4_SC_AT)
+        nc.vector.memset(w4_sc[:], 0)
         for r in range(4):
-            nc.gpsimd.dma_start(
+            nc.sync.dma_start(
                 w4_sc[r:P:32, :, :], w4_scales[:, r:16:4, :].rearrange("a q n -> q a n").bitcast(I32)
             )
-        b_rows = keep.tile([P, P], F32, name="b_rows")
-        ident = keep.tile([P, P], F32, name="ident")
-        nc.gpsimd.memset(b_rows[:], 0.0)
-        nc.gpsimd.dma_start(b_rows[0:ROW_TILES, :], b.rearrange("(m p) -> m p", p=P))
-        make_identity(nc, ident[:])
 
-        v_codes0 = keep.tile([P, S], U32, name="v_codes0", align_bytes=64)
+        v_codes0 = [keep.tile([P, CHUNK], U32, name="v_codes0_%d" % c, align_bytes=64) for c in range(CHUNKS - 1)]
+        v_codes0.append(placed([P, CHUNK], U32, "v_codes0_last", V0_LAST_AT))
         v_codes1 = [placed([P, CHUNK], U32, "v_codes1_%d" % c, V1_AT + 2 * c) for c in range(CHUNKS)]
         down_codes = placed([P, PASSES, R], U32, "down_codes", DOWN_CODES_AT)
         down_sc = placed([P, PASSES, R], U8, "down_sc", DOWN_SC_AT)
-        up_codes = [placed([P, UP_PART], U32, "up_codes%d" % part, UP_CODES_AT[part]) for part in range(M // UP_PART)]
+        up_codes = []
         up_sc = keep.tile([P, M], U8, name="up_sc", align_bytes=64)
         h_codes = keep.tile([P, S], U32, name="h_codes", align_bytes=64)
         h_sc = keep.tile([P, S], U8, name="h_sc", align_bytes=64)
 
         def v_codes(a, j0, j1):
-            if a == 0:
-                return v_codes0[:, j0:j1]
             c = j0 // CHUNK
-            return v_codes1[c][:, j0 - c * CHUNK : j1 - c * CHUNK]
+            return (v_codes0, v_codes1)[a][c][:, j0 - c * CHUNK : j1 - c * CHUNK]
 
         def gather_words(a, j0, j1):
             nc.vector.tensor_copy(v_codes(a, j0, j1), words[a][:].bitcast(U32).indirect(entries(j0, j1)))
 
         def quantize_down(a):
-            grouped = placed([P, PACK * R], BF16, "down_grouped%d" % a, V1_AT + 4 * (1 - a))
+            grouped = placed([P, PACK * R], BF16, "down_grouped%d" % a, DOWN_GROUPED_AT[a])
             nc.scalar.copy(
                 grouped[:].rearrange("p (t m i) -> p m i t", t=PACK, i=PACK),
                 down_raw[a][:].rearrange("p i (m t) -> p m i t", t=PACK),
@@ -148,13 +164,15 @@ def tile_list_tabgate_bias_kernel(
                 grouped.rearrange("p (c n i) -> p c i n", n=PACK, i=PACK),
                 raw.rearrange("p i (c n) -> p c i n", n=PACK),
             )
-            nc.vector.quantize_mx(up_codes[part][:].bitcast(FP8X4), up_sc[:, cols], grouped)
+            codes = placed([P, UP_PART], U32, "up_codes%d" % part, UP_CODES_AT[part])
+            nc.vector.quantize_mx(codes[:].bitcast(FP8X4), up_sc[:, cols], grouped)
+            up_codes.append(codes)
 
         def make_h(c):
             grouped = placed([P, PACK * CHUNK], BF16, "h_grouped%d" % c, H_GROUPED_AT[c])
             for blk in range(CHUNK // BLOCK):
                 j0 = c * CHUNK + blk * BLOCK
-                bank = psum_h.tile([P, PACK, BLOCK], F32, name="h_bank", tag="h_bank")
+                bank = psum.tile([P, PACK, BLOCK], F32, name="h_bank", tag="bank")
                 for a in range(PASSES):
                     for t in range(PACK):
                         nc.tensor.matmul_mx(
@@ -166,7 +184,8 @@ def tile_list_tabgate_bias_kernel(
                             start=(a == 0 and t == 0),
                             stop=(a == PASSES - 1 and t == PACK - 1),
                         )
-                nc.scalar.copy(
+                copy = nc.vector.tensor_copy if j0 // BLOCK in H_BLOCKS_ON_VECTOR else nc.scalar.copy
+                copy(
                     grouped[:, PACK * BLOCK * blk : PACK * BLOCK * (blk + 1)].rearrange("p (n t) -> p n t", t=PACK),
                     bank[:].rearrange("p t n -> p n t"),
                 )
@@ -178,7 +197,7 @@ def tile_list_tabgate_bias_kernel(
             y = ypool.tile([P, j_end - j_start], F32, name="y")
             for u in range((j_end - j_start) // CHUNK):
                 cols = slice(j_start + u * CHUNK, j_start + (u + 1) * CHUNK)
-                bank = psum_y.tile([P, CHUNK], F32, name="y_bank", tag="y_bank")
+                bank = psum.tile([P, CHUNK], F32, name="y_bank", tag="bank")
                 nc.tensor.matmul_mx(
                     bank[:],
                     lhsT=up_codes[m // 2][:, (m % 2) * P : (m % 2 + 1) * P].bitcast(FP8X4),
@@ -198,7 +217,7 @@ def tile_list_tabgate_bias_kernel(
                         start=False,
                         stop=(a == PASSES - 1),
                     )
-                nc.scalar.activation(y[:, u * CHUNK : (u + 1) * CHUNK], bank[:], IDENTITY, bias=bias[:, m : m + 1])
+                nc.scalar.activation(y[:, u * CHUNK : (u + 1) * CHUNK], bank[:], IDENTITY, bias=bias[m])
             nc.vector.tensor_tensor(
                 result[:, j_start:j_end], gates[m][:].indirect(entries(j_start, j_end)), y[:], MULT
             )
@@ -206,35 +225,32 @@ def tile_list_tabgate_bias_kernel(
         def result_tile(m):
             return placed([P, S], F32, "result%d" % m, RESULT_AT[m])
 
-        gather_words(0, 0, S)
+        for c in range(CHUNKS - 1):
+            gather_words(0, c * CHUNK, (c + 1) * CHUNK)
+        quantize_down(0)
+        gather_words(0, S - CHUNK, S)
         w4 = placed([P, PASSES, 2 * M // 4], I32, "w4", W4_AT)
         nc.sync.dma_start(w4[:], w4_words.rearrange("a p c -> p a c").bitcast(I32))
         load_gate(0)
-        for a in range(PASSES):
-            quantize_down(a)
+        quantize_down(1)
         load_gate(1)
-        for c in range(CHUNKS - 1):
+        for c in range(CHUNKS):
             gather_words(1, c * CHUNK, (c + 1) * CHUNK)
         make_h(0)
         load_gate(2)
-        gather_words(1, S - CHUNK, S)
         load_gate(3)
-        quantize_up(0)
-        b_psum = psum_y.tile([P, P], F32, name="b_psum", tag="y_bank")
-        nc.tensor.transpose(b_psum[:], b_rows[:], ident[:])
-        bias = keep.tile([P, ROW_TILES], F32, name="bias")
-        nc.scalar.copy(bias[:], b_psum[:, 0:ROW_TILES])
         make_h(1)
         load_gate(4)
+        quantize_up(0)
+        make_h(2)
+        load_gate(5)
+        make_h(3)
+        load_gate(6)
+        load_gate(7)
         result = result_tile(0)
         for c in range(CHUNKS):
             gated(0, result, c * CHUNK, (c + 1) * CHUNK)
-            if c + 2 < CHUNKS:
-                make_h(c + 2)
-                load_gate(c + 5)
-            if c == 1:
-                load_gate(7)
-                quantize_up(1)
+        quantize_up(1)
         nc.sync.dma_start(out[0:P, :], result[:])
 
         for m in range(1, ROW_TILES):
@@ -246,7 +262,7 @@ def tile_list_tabgate_bias_kernel(
                 gated(m, result, j_start, j_end)
                 if last:
                     nc.sync.dma_start(out[rows, j_start:j_end], result[:, j_start:j_end])
-            if m in (1, 3):
-                quantize_up((m + 3) // 2)
+            if m < early:
+                quantize_up(m + 1)
             if not last:
                 nc.sync.dma_start(out[rows, :], result[:])

@@ -256,13 +256,8 @@ def tile_list_tabgate_bias_kernel(
         for m in range(1, ROW_TILES):
             rows = slice(m * P, (m + 1) * P)
             result = result_tile(m)
-            last = m == ROW_TILES - 1
-            edges = (0, 2 * CHUNK, 3 * CHUNK, S) if last else (0, 2 * CHUNK, S)
-            for j_start, j_end in zip(edges, edges[1:]):
-                gated(m, result, j_start, j_end)
-                if last:
-                    nc.sync.dma_start(out[rows, j_start:j_end], result[:, j_start:j_end])
+            for j_start in (0, S // 2):
+                gated(m, result, j_start, j_start + S // 2)
             if m < early:
                 quantize_up(m + 1)
-            if not last:
-                nc.sync.dma_start(out[rows, :], result[:])
+            nc.sync.dma_start(out[rows, :], result[:])

@@ -27,7 +27,7 @@ ROW_TILES = M // P
 LIST_ROWS = 16
 UP_PART = 256
 GATE_AT = (52, 68, 92, 0, 108, 124, 140, 156)
-WORDS_AT = (37, 0)
+WORDS_AT = (38, 0)
 TAB_SC_AT = 15
 UP_AT = 18
 W4_AT = 34
@@ -43,6 +43,7 @@ DOWN_SC_AT = 184
 UP_GROUPED_AT = (172, 188, 190, 192)
 H_GROUPED_AT = (92, 108, 124, 154)
 H_BLOCKS_ON_VECTOR = (8, 9, 10, 13)
+LAST_CUTS = (0, 1024, 1536, 2048)
 RESULT_AT = (172, 180, 52, 60, 68, 76, 92, 100)
 
 
@@ -66,10 +67,19 @@ def tile_list_tabgate_bias_kernel(
             return offsets[:, j0 // LIST_ROWS : j1 // LIST_ROWS]
 
         tab_sc = placed([P, T // 4], I32, "tab_sc", TAB_SC_AT)
-        nc.sync.dma_start(tab_sc[0:32, :], tab_scales.rearrange("a q t -> (a q) t").bitcast(I32))
+        nc.vector.memset(tab_sc[:], 0)
+
+        def load_down(a):
+            raw = placed([P, PACK, R], F32, "down_raw%d" % a, DOWN_AT[a])
+            nc.sync.dma_start(raw[:], down.rearrange("(a p i) r -> a p i r", p=P, i=PACK)[a])
+            return raw
+
+        w4 = placed([P, PASSES, 2 * M // 4], I32, "w4", W4_AT)
+        nc.sync.dma_start(w4[:], w4_words.rearrange("a p c -> p a c").bitcast(I32))
         b_rows = keep.tile([P, P], F32, name="b_rows")
         ident = keep.tile([P, P], F32, name="ident")
         nc.sync.dma_start(b_rows[B_ROW : B_ROW + ROW_TILES, :], b.rearrange("(m p) -> m p", p=P))
+        nc.sync.dma_start(tab_sc[32:96:2, :], tab_scales.rearrange("a q t -> (a q) t").bitcast(I32))
         nc.gpsimd.memset(b_rows[0:B_ROW, :], 0.0)
         nc.gpsimd.memset(b_rows[32:64, :], 0.0)
         nc.gpsimd.memset(b_rows[64:128, :], 0.0)
@@ -85,18 +95,11 @@ def tile_list_tabgate_bias_kernel(
         late_bias = keep.tile([P, ROW_TILES - early], F32, name="late_bias")
         nc.scalar.copy(late_bias[:], b_psum[:, B_ROW + early : B_ROW + ROW_TILES])
         bias.extend(late_bias[:, m : m + 1] for m in range(ROW_TILES - early))
-        nc.vector.memset(tab_sc[64:128, :], 0)
-        nc.vector.memset(tab_sc[32:64, :], 0)
 
         def load_words(a):
             window = placed([P, T], I32, "window%d" % a, WORDS_AT[a])
             nc.sync.dma_start(window[:], tab_words[a].rearrange("p t i -> p (t i)").bitcast(I32))
             return window
-
-        def load_down(a):
-            raw = placed([P, PACK, R], F32, "down_raw%d" % a, DOWN_AT[a])
-            nc.sync.dma_start(raw[:], down.rearrange("(a p i) r -> a p i r", p=P, i=PACK)[a])
-            return raw
 
         gates = []
 
@@ -116,7 +119,7 @@ def tile_list_tabgate_bias_kernel(
             plane = keep.tile([P, S // 4], I32, name="v_sc%d" % a, align_bytes=64)
             nc.vector.memset(plane[:], 0)
             for r in range(4):
-                nc.sync.dma_start(plane[r:P:32, :], picked_sc[16 * a + r : 16 * (a + 1) : 4, :].bitcast(I32))
+                nc.sync.dma_start(plane[r:P:32, :], picked_sc[32 + 32 * a + 2 * r : 64 + 32 * a : 8, :].bitcast(I32))
             v_sc.append(plane[:].bitcast(U8))
 
         place_scales(0)
@@ -229,8 +232,6 @@ def tile_list_tabgate_bias_kernel(
             gather_words(0, c * CHUNK, (c + 1) * CHUNK)
         quantize_down(0)
         gather_words(0, S - CHUNK, S)
-        w4 = placed([P, PASSES, 2 * M // 4], I32, "w4", W4_AT)
-        nc.sync.dma_start(w4[:], w4_words.rearrange("a p c -> p a c").bitcast(I32))
         load_gate(0)
         quantize_down(1)
         load_gate(1)
@@ -253,7 +254,7 @@ def tile_list_tabgate_bias_kernel(
         quantize_up(1)
         nc.sync.dma_start(out[0:P, :], result[:])
 
-        for m in range(1, ROW_TILES):
+        for m in range(1, ROW_TILES - 1):
             rows = slice(m * P, (m + 1) * P)
             result = result_tile(m)
             for j_start in (0, S // 2):
@@ -261,3 +262,8 @@ def tile_list_tabgate_bias_kernel(
             if m < early:
                 quantize_up(m + 1)
             nc.sync.dma_start(out[rows, :], result[:])
+        m = ROW_TILES - 1
+        result = result_tile(m)
+        for j0, j1 in zip(LAST_CUTS, LAST_CUTS[1:]):
+            gated(m, result, j0, j1)
+            nc.sync.dma_start(out[m * P : (m + 1) * P, j0:j1], result[:, j0:j1])

@@ -58,7 +58,7 @@ def tile_list_tabgate_bias_kernel(
         psum = ctx.enter_context(tc.psum_pool(name="psum", bufs=8))
 
         def placed(shape, dtype, name, kib):
-            return space.tile(shape, dtype, name=name, offset=kib * 1024, align_bytes=64)
+            return space.tile(shape, dtype, name=name, offset=kib * 1024, align_bytes=256)
 
         offsets = keep.tile([P, S // LIST_ROWS], U16, name="offsets")
         nc.sync.dma_start(offsets[:], offs)
@@ -111,12 +111,12 @@ def tile_list_tabgate_bias_kernel(
         words = [load_words(0)]
         down_raw = [load_down(a) for a in range(PASSES)]
 
-        picked_sc = keep.tile([P, S], U8, name="picked_sc", align_bytes=64)
+        picked_sc = keep.tile([P, S], U8, name="picked_sc", align_bytes=256)
         nc.vector.tensor_copy(picked_sc[:], tab_sc[:].bitcast(U8).indirect(offsets[:]))
         v_sc = []
 
         def place_scales(a):
-            plane = keep.tile([P, S // 4], I32, name="v_sc%d" % a, align_bytes=64)
+            plane = keep.tile([P, S // 4], I32, name="v_sc%d" % a, align_bytes=256)
             nc.vector.memset(plane[:], 0)
             for r in range(4):
                 nc.sync.dma_start(plane[r:P:32, :], picked_sc[32 + 32 * a + 2 * r : 64 + 32 * a : 8, :].bitcast(I32))

@@ -67,7 +67,9 @@ def tile_list_tabgate_bias_kernel(
             return offsets[:, j0 // LIST_ROWS : j1 // LIST_ROWS]
 
         tab_sc = placed([P, T // 4], I32, "tab_sc", TAB_SC_AT)
-        nc.vector.memset(tab_sc[:], 0)
+        nc.sync.dma_start(tab_sc[32:64, :], tab_scales.rearrange("a q t -> (a q) t").bitcast(I32))
+        nc.vector.memset(tab_sc[0:32, :], 0)
+        nc.vector.memset(tab_sc[64:P, :], 0)
 
         def load_down(a):
             raw = placed([P, PACK, R], F32, "down_raw%d" % a, DOWN_AT[a])
@@ -79,7 +81,6 @@ def tile_list_tabgate_bias_kernel(
         b_rows = keep.tile([P, P], F32, name="b_rows")
         ident = keep.tile([P, P], F32, name="ident")
         nc.sync.dma_start(b_rows[B_ROW : B_ROW + ROW_TILES, :], b.rearrange("(m p) -> m p", p=P))
-        nc.sync.dma_start(tab_sc[32:96:2, :], tab_scales.rearrange("a q t -> (a q) t").bitcast(I32))
         nc.gpsimd.memset(b_rows[0:B_ROW, :], 0.0)
         nc.gpsimd.memset(b_rows[32:64, :], 0.0)
         nc.gpsimd.memset(b_rows[64:128, :], 0.0)
@@ -119,7 +120,7 @@ def tile_list_tabgate_bias_kernel(
             plane = keep.tile([P, S // 4], I32, name="v_sc%d" % a, align_bytes=256)
             nc.vector.memset(plane[:], 0)
             for r in range(4):
-                nc.sync.dma_start(plane[r:P:32, :], picked_sc[32 + 32 * a + 2 * r : 64 + 32 * a : 8, :].bitcast(I32))
+                nc.sync.dma_start(plane[r:P:32, :], picked_sc[32 + 16 * a + r : 48 + 16 * a : 4, :].bitcast(I32))
             v_sc.append(plane[:].bitcast(U8))
 
         place_scales(0)

@@ -1,7 +1,6 @@
 from contextlib import ExitStack
 
 import concourse.mybir as mybir
-from concourse.masks import make_identity
 
 K, M, T, S, R = 1024, 1024, 4096, 2048, 512
 FLOPS = 2 * S * (K * M + K * R + R * M)
@@ -23,28 +22,35 @@ PASSES = K // (P * PACK)
 CHUNK = 512
 CHUNKS = S // CHUNK
 BLOCK = 128
-ROW_TILES = M // P
+ROWS = M // P
 LIST_ROWS = 16
-UP_PART = 256
-GATE_AT = (52, 68, 92, 0, 108, 124, 140, 156)
-WORDS_AT = (38, 0)
-TAB_SC_AT = 15
-UP_AT = 18
-W4_AT = 34
-DOWN_CODES_AT = 180
-W4_SC_AT = 16
-DOWN_AT = (68, 76)
-V1_AT = 84
-V0_LAST_AT = 194
-DOWN_GROUPED_AT = (V0_LAST_AT, V1_AT)
-UP_CODES_AT = (43, 60, 76, 100)
-B_ROW = 24
-DOWN_SC_AT = 184
-UP_GROUPED_AT = (172, 188, 190, 192)
-H_GROUPED_AT = (92, 108, 124, 154)
+UP_ROWS = 2
+GATE_AT = (0, 16, 218, 32, 48, 64, 80, 96)
+WORDS_AT = (0, 218)
+DOWN_AT = (16, 24)
+H_GROUPED_AT = (32, 62, 94, 234)
+UP_GROUPED_AT = (120, 234, 236, 234)
+W4_RAW_AT = 112
+W4_SC_RAW_AT = 116
+PICKED_AT = 118
+DOWN_GROUPED_AT = (196, 124)
+DOWN_CODES_AT = 128
+DOWN_SC_AT = 132
+Y_AT = (144, 152)
+V_AT = (160, 168)
+H_CODES_AT = 176
+W4_AT = 184
+UP_CODES_AT = 188
+V_SC_AT = (192, 194)
+H_SC_AT = 196
+UP_SC_AT = 201
+BIAS_AT = 200
+UP_RAW_AT = 202
+TAB_SC_AT = 216
+W4_SC_AT = 198
 H_BLOCKS_ON_VECTOR = (8, 9, 10, 13)
+STORES = ((0, 4, 112), (4, 6, 0), (6, 7, 16), (7, 8, 24))
 LAST_CUTS = (0, 1024, 1536, 2048)
-RESULT_AT = (172, 180, 52, 60, 68, 76, 92, 100)
 
 
 def tile_list_tabgate_bias_kernel(
@@ -54,7 +60,6 @@ def tile_list_tabgate_bias_kernel(
     with ExitStack() as ctx:
         keep = ctx.enter_context(tc.tile_pool(name="keep", bufs=1))
         space = ctx.enter_context(tc.tile_pool(name="space", bufs=1))
-        ypool = ctx.enter_context(tc.tile_pool(name="ypool", bufs=4))
         psum = ctx.enter_context(tc.psum_pool(name="psum", bufs=8))
 
         def placed(shape, dtype, name, kib):
@@ -67,90 +72,73 @@ def tile_list_tabgate_bias_kernel(
             return offsets[:, j0 // LIST_ROWS : j1 // LIST_ROWS]
 
         tab_sc = placed([P, T // 4], I32, "tab_sc", TAB_SC_AT)
-        nc.sync.dma_start(tab_sc[32:64, :], tab_scales.rearrange("a q t -> (a q) t").bitcast(I32))
-        nc.vector.memset(tab_sc[0:32, :], 0)
-        nc.vector.memset(tab_sc[64:P, :], 0)
+        nc.vector.memset(tab_sc[:], 0)
+        w4_sc_raw = placed([P, PASSES, M // 4], I32, "w4_sc_raw", W4_SC_RAW_AT)
+        nc.vector.memset(w4_sc_raw[:], 0)
 
-        def load_down(a):
-            raw = placed([P, PACK, R], F32, "down_raw%d" % a, DOWN_AT[a])
-            nc.sync.dma_start(raw[:], down.rearrange("(a p i) r -> a p i r", p=P, i=PACK)[a])
-            return raw
-
-        w4 = placed([P, PASSES, 2 * M // 4], I32, "w4", W4_AT)
-        nc.sync.dma_start(w4[:], w4_words.rearrange("a p c -> p a c").bitcast(I32))
-        b_rows = keep.tile([P, P], F32, name="b_rows")
-        ident = keep.tile([P, P], F32, name="ident")
-        nc.sync.dma_start(b_rows[B_ROW : B_ROW + ROW_TILES, :], b.rearrange("(m p) -> m p", p=P))
-        nc.gpsimd.memset(b_rows[0:B_ROW, :], 0.0)
-        nc.gpsimd.memset(b_rows[32:64, :], 0.0)
-        nc.gpsimd.memset(b_rows[64:128, :], 0.0)
-        make_identity(nc, ident[:])
-        b_psum = psum.tile([P, P], F32, name="b_psum", tag="bank")
-        nc.tensor.transpose(b_psum[:], b_rows[:], ident[:])
-        early = len(UP_GROUPED_AT) - 1
-        bias = []
-        for m in range(early):
-            column = placed([P, 1], F32, "bias%d" % m, UP_GROUPED_AT[m + 1])
-            nc.scalar.copy(column[:], b_psum[:, B_ROW + m : B_ROW + m + 1])
-            bias.append(column[:])
-        late_bias = keep.tile([P, ROW_TILES - early], F32, name="late_bias")
-        nc.scalar.copy(late_bias[:], b_psum[:, B_ROW + early : B_ROW + ROW_TILES])
-        bias.extend(late_bias[:, m : m + 1] for m in range(ROW_TILES - early))
+        w4_raw = placed([P, PASSES, 2 * M // 4], I32, "w4_raw", W4_RAW_AT)
+        nc.sync.dma_start(w4_raw[:], w4_words.rearrange("a p c -> p a c").bitcast(I32))
+        bias = placed([P, ROWS], F32, "bias", BIAS_AT)
+        nc.sync.dma_start(bias[:], b.rearrange("(p u) -> p u", u=ROWS))
+        nc.sync.dma_start(tab_sc[32:96:2, :], tab_scales.rearrange("a q t -> (a q) t").bitcast(I32))
+        for r in range(4):
+            nc.gpsimd.dma_start(
+                w4_sc_raw[r:P:32, :, :], w4_scales[:, r:16:4, :].rearrange("a q n -> q a n").bitcast(I32)
+            )
 
         def load_words(a):
             window = placed([P, T], I32, "window%d" % a, WORDS_AT[a])
             nc.sync.dma_start(window[:], tab_words[a].rearrange("p t i -> p (t i)").bitcast(I32))
             return window
 
-        gates = []
-
-        def load_gate(m):
-            gate = placed([P, T], F32, "gate%d" % m, GATE_AT[m])
-            nc.sync.dma_start(gate[:], gT[m * P : (m + 1) * P, :])
-            gates.append(gate)
+        def load_down(a):
+            raw = placed([P, PACK, R], F32, "down_raw%d" % a, DOWN_AT[a])
+            nc.sync.dma_start(raw[:], down.rearrange("(a p i) r -> a p i r", p=P, i=PACK)[a])
+            return raw
 
         words = [load_words(0)]
         down_raw = [load_down(a) for a in range(PASSES)]
 
-        picked_sc = keep.tile([P, S], U8, name="picked_sc", align_bytes=256)
+        picked_sc = placed([P, S], U8, "picked_sc", PICKED_AT)
         nc.vector.tensor_copy(picked_sc[:], tab_sc[:].bitcast(U8).indirect(offsets[:]))
         v_sc = []
 
         def place_scales(a):
-            plane = keep.tile([P, S // 4], I32, name="v_sc%d" % a, align_bytes=256)
+            plane = placed([P, S // 4], I32, "v_sc%d" % a, V_SC_AT[a])
             nc.vector.memset(plane[:], 0)
             for r in range(4):
-                nc.sync.dma_start(plane[r:P:32, :], picked_sc[32 + 16 * a + r : 48 + 16 * a : 4, :].bitcast(I32))
+                first = 32 + 32 * a + 2 * r
+                nc.sync.dma_start(plane[r:P:32, :], picked_sc[first : first + 32 - 2 * r : 8, :].bitcast(I32))
             v_sc.append(plane[:].bitcast(U8))
 
         place_scales(0)
         words.append(load_words(1))
         place_scales(1)
-        up_raw = placed([P, PACK, M], F32, "up_raw", UP_AT)
+        up_raw = placed([P, PACK, M], F32, "up_raw", UP_RAW_AT)
         nc.sync.dma_start(up_raw[:], up.rearrange("(p i) n -> p i n", i=PACK))
-        w4_sc = placed([P, PASSES, M // 4], I32, "w4_sc", W4_SC_AT)
-        nc.vector.memset(w4_sc[:], 0)
-        for r in range(4):
-            nc.sync.dma_start(
-                w4_sc[r:P:32, :, :], w4_scales[:, r:16:4, :].rearrange("a q n -> q a n").bitcast(I32)
+
+        w4 = placed([P, PASSES, ROWS, P], U16, "w4", W4_AT)
+        for u0 in range(0, ROWS, 4):
+            nc.scalar.copy(
+                w4[:, :, u0 : u0 + 4, :].rearrange("p a u c -> p a c u"),
+                w4_raw[:].bitcast(U16).rearrange("p a (c u) -> p a c u", u=ROWS)[:, :, :, u0 : u0 + 4],
             )
 
-        v_codes0 = [keep.tile([P, CHUNK], U32, name="v_codes0_%d" % c, align_bytes=64) for c in range(CHUNKS - 1)]
-        v_codes0.append(placed([P, CHUNK], U32, "v_codes0_last", V0_LAST_AT))
-        v_codes1 = [placed([P, CHUNK], U32, "v_codes1_%d" % c, V1_AT + 2 * c) for c in range(CHUNKS)]
+        v_codes = [
+            [placed([P, CHUNK], U32, "v_codes%d_%d" % (a, c), V_AT[a] + 2 * c) for c in range(CHUNKS)]
+            for a in range(PASSES)
+        ]
         down_codes = placed([P, PASSES, R], U32, "down_codes", DOWN_CODES_AT)
         down_sc = placed([P, PASSES, R], U8, "down_sc", DOWN_SC_AT)
-        up_codes = []
-        up_sc = keep.tile([P, M], U8, name="up_sc", align_bytes=64)
-        h_codes = keep.tile([P, S], U32, name="h_codes", align_bytes=64)
-        h_sc = keep.tile([P, S], U8, name="h_sc", align_bytes=64)
+        up_codes = placed([P, M], U32, "up_codes", UP_CODES_AT)
+        up_sc = placed([P, M], U8, "up_sc", UP_SC_AT)
+        h_codes = placed([P, S], U32, "h_codes", H_CODES_AT)
+        h_sc = placed([P, S], U8, "h_sc", H_SC_AT)
 
-        def v_codes(a, j0, j1):
-            c = j0 // CHUNK
-            return (v_codes0, v_codes1)[a][c][:, j0 - c * CHUNK : j1 - c * CHUNK]
-
-        def gather_words(a, j0, j1):
-            nc.vector.tensor_copy(v_codes(a, j0, j1), words[a][:].bitcast(U32).indirect(entries(j0, j1)))
+        def gather_words(a, c):
+            nc.vector.tensor_copy(
+                v_codes[a][c][:], words[a][:].bitcast(U32).indirect(entries(c * CHUNK, (c + 1) * CHUNK))
+            )
 
         def quantize_down(a):
             grouped = placed([P, PACK * R], BF16, "down_grouped%d" % a, DOWN_GROUPED_AT[a])
@@ -161,21 +149,20 @@ def tile_list_tabgate_bias_kernel(
             nc.vector.quantize_mx(down_codes[:, a, :].bitcast(FP8X4), down_sc[:, a, :], grouped[:])
 
         def quantize_up(part):
-            cols = slice(part * UP_PART, (part + 1) * UP_PART)
-            raw = up_raw[:, :, cols]
-            grouped = placed([P, PACK * UP_PART], BF16, "up_grouped%d" % part, UP_GROUPED_AT[part])[:]
+            u0 = part * UP_ROWS
+            cols = slice(u0 * P, (u0 + UP_ROWS) * P)
+            grouped = placed([P, PACK * UP_ROWS * P], BF16, "up_grouped%d" % part, UP_GROUPED_AT[part])
             nc.scalar.copy(
-                grouped.rearrange("p (c n i) -> p c i n", n=PACK, i=PACK),
-                raw.rearrange("p i (c n) -> p c i n", n=PACK),
+                grouped[:].rearrange("p (u c i) -> p c u i", u=UP_ROWS, i=PACK),
+                up_raw[:].rearrange("p i (c u) -> p c u i", u=ROWS)[:, :, u0 : u0 + UP_ROWS, :],
             )
-            codes = placed([P, UP_PART], U32, "up_codes%d" % part, UP_CODES_AT[part])
-            nc.vector.quantize_mx(codes[:].bitcast(FP8X4), up_sc[:, cols], grouped)
-            up_codes.append(codes)
+            nc.vector.quantize_mx(up_codes[:, cols].bitcast(FP8X4), up_sc[:, cols], grouped[:])
 
         def make_h(c):
             grouped = placed([P, PACK * CHUNK], BF16, "h_grouped%d" % c, H_GROUPED_AT[c])
             for blk in range(CHUNK // BLOCK):
                 j0 = c * CHUNK + blk * BLOCK
+                cols = slice(blk * BLOCK, (blk + 1) * BLOCK)
                 bank = psum.tile([P, PACK, BLOCK], F32, name="h_bank", tag="bank")
                 for a in range(PASSES):
                     for t in range(PACK):
@@ -183,7 +170,7 @@ def tile_list_tabgate_bias_kernel(
                             bank[:, t, :],
                             lhsT=down_codes[:, a, t * P : (t + 1) * P].bitcast(FP8X4),
                             lhsT_scale=down_sc[:, a, t * P : (t + 1) * P],
-                            rhs=v_codes(a, j0, j0 + BLOCK).bitcast(FP8X4),
+                            rhs=v_codes[a][c][:, cols].bitcast(FP8X4),
                             rhs_scale=v_sc[a][:, j0 : j0 + BLOCK],
                             start=(a == 0 and t == 0),
                             stop=(a == PASSES - 1 and t == PACK - 1),
@@ -196,75 +183,83 @@ def tile_list_tabgate_bias_kernel(
             cols = slice(c * CHUNK, (c + 1) * CHUNK)
             nc.vector.quantize_mx(h_codes[:, cols].bitcast(FP8X4), h_sc[:, cols], grouped[:])
 
-        def gated(m, result, j_start, j_end):
-            rows = slice(m * P, (m + 1) * P)
-            y = ypool.tile([P, j_end - j_start], F32, name="y")
-            for u in range((j_end - j_start) // CHUNK):
-                cols = slice(j_start + u * CHUNK, j_start + (u + 1) * CHUNK)
+        gates = []
+
+        def load_gate(u):
+            gate = placed([P, T], F32, "gate%d" % u, GATE_AT[u])
+            nc.sync.dma_start(gate[:], gT.rearrange("(p u) t -> u p t", u=ROWS)[u])
+            gates.append(gate)
+
+        def make_y(u):
+            y = placed([P, S], F32, "y%d" % u, Y_AT[u % 2])
+            for c in range(CHUNKS):
+                cols = slice(c * CHUNK, (c + 1) * CHUNK)
                 bank = psum.tile([P, CHUNK], F32, name="y_bank", tag="bank")
-                nc.tensor.matmul_mx(
-                    bank[:],
-                    lhsT=up_codes[m // 2][:, (m % 2) * P : (m % 2 + 1) * P].bitcast(FP8X4),
-                    lhsT_scale=up_sc[:, rows],
-                    rhs=h_codes[:, cols].bitcast(FP8X4),
-                    rhs_scale=h_sc[:, cols],
-                    start=True,
-                    stop=False,
-                )
                 for a in range(PASSES):
                     nc.tensor.matmul_mx(
                         bank[:],
-                        lhsT=w4[:, a, :].bitcast(U8)[:, 2 * m * P : 2 * (m + 1) * P].bitcast(FP4X4),
-                        lhsT_scale=w4_sc[:, a, :].bitcast(U8)[:, rows],
-                        rhs=v_codes(a, cols.start, cols.stop).bitcast(FP8X4),
+                        lhsT=w4[:, a, u, :].bitcast(U8).bitcast(FP4X4),
+                        lhsT_scale=w4_sc[:, a, u, :],
+                        rhs=v_codes[a][c][:].bitcast(FP8X4),
                         rhs_scale=v_sc[a][:, cols],
-                        start=False,
-                        stop=(a == PASSES - 1),
+                        start=(a == 0),
+                        stop=False,
                     )
-                nc.scalar.activation(y[:, u * CHUNK : (u + 1) * CHUNK], bank[:], IDENTITY, bias=bias[m])
-            nc.vector.tensor_tensor(
-                result[:, j_start:j_end], gates[m][:].indirect(entries(j_start, j_end)), y[:], MULT
-            )
+                nc.tensor.matmul_mx(
+                    bank[:],
+                    lhsT=up_codes[:, u * P : (u + 1) * P].bitcast(FP8X4),
+                    lhsT_scale=up_sc[:, u * P : (u + 1) * P],
+                    rhs=h_codes[:, cols].bitcast(FP8X4),
+                    rhs_scale=h_sc[:, cols],
+                    start=False,
+                    stop=True,
+                )
+                nc.scalar.activation(y[:, cols], bank[:], IDENTITY, bias=bias[:, u : u + 1])
+            return y
 
-        def result_tile(m):
-            return placed([P, S], F32, "result%d" % m, RESULT_AT[m])
+        def gate_cols(u, y, result, j0, j1):
+            nc.vector.tensor_tensor(result[:, j0:j1], gates[u][:].indirect(entries(j0, j1)), y[:, j0:j1], MULT)
 
-        for c in range(CHUNKS - 1):
-            gather_words(0, c * CHUNK, (c + 1) * CHUNK)
-        quantize_down(0)
-        gather_words(0, S - CHUNK, S)
+        for c in range(CHUNKS):
+            gather_words(0, c)
         load_gate(0)
+        quantize_down(0)
         quantize_down(1)
         load_gate(1)
+        w4_sc = placed([P, PASSES, ROWS, P], U8, "w4_sc", W4_SC_AT)
+        nc.vector.tensor_copy(w4_sc[:], w4_sc_raw[:].bitcast(U8).rearrange("p a (c u) -> p a u c", u=ROWS))
         for c in range(CHUNKS):
-            gather_words(1, c * CHUNK, (c + 1) * CHUNK)
-        make_h(0)
+            gather_words(1, c)
         load_gate(2)
+        make_h(0)
         load_gate(3)
         make_h(1)
         load_gate(4)
+        load_gate(5)
         quantize_up(0)
         make_h(2)
-        load_gate(5)
-        make_h(3)
         load_gate(6)
         load_gate(7)
-        result = result_tile(0)
-        for c in range(CHUNKS):
-            gated(0, result, c * CHUNK, (c + 1) * CHUNK)
-        quantize_up(1)
-        nc.sync.dma_start(out[0:P, :], result[:])
+        make_h(3)
 
-        for m in range(1, ROW_TILES - 1):
-            rows = slice(m * P, (m + 1) * P)
-            result = result_tile(m)
-            for j_start in (0, S // 2):
-                gated(m, result, j_start, j_start + S // 2)
-            if m < early:
-                quantize_up(m + 1)
-            nc.sync.dma_start(out[rows, :], result[:])
-        m = ROW_TILES - 1
-        result = result_tile(m)
-        for j0, j1 in zip(LAST_CUTS, LAST_CUTS[1:]):
-            gated(m, result, j0, j1)
-            nc.sync.dma_start(out[m * P : (m + 1) * P, j0:j1], result[:, j0:j1])
+        out_rows = out.rearrange("(p u) j -> p u j", u=ROWS)
+        for u0, u1, at in STORES:
+            result = placed([P, u1 - u0, S], F32, "result%d" % u0, at)
+            for u in range(u0, u1):
+                y = make_y(u)
+                if u == 0:
+                    cuts = range(0, S + 1, CHUNK)
+                elif u == 1:
+                    cuts = range(0, S + 1, S // 2)
+                elif u == ROWS - 1:
+                    cuts = LAST_CUTS
+                else:
+                    cuts = (0, S)
+                for j0, j1 in zip(cuts, cuts[1:]):
+                    gate_cols(u, y, result[:, u - u0, :], j0, j1)
+                    if u == ROWS - 1:
+                        nc.sync.dma_start(out_rows[:, u, j0:j1], result[:, u - u0, j0:j1])
+                if u + 1 < ROWS // UP_ROWS:
+                    quantize_up(u + 1)
+            if u1 < ROWS:
+                nc.sync.dma_start(out_rows[:, u0:u1, :], result[:])

@@ -25,18 +25,18 @@ BLOCK = 128
 ROWS = M // P
 LIST_ROWS = 16
 UP_ROWS = 2
-GATE_AT = (0, 16, 218, 32, 48, 64, 80, 96)
-WORDS_AT = (0, 218)
-DOWN_AT = (16, 24)
-H_GROUPED_AT = (32, 62, 94, 234)
-UP_GROUPED_AT = (120, 234, 236, 234)
-W4_RAW_AT = 112
-W4_SC_RAW_AT = 116
-PICKED_AT = 118
-DOWN_GROUPED_AT = (196, 124)
-DOWN_CODES_AT = 128
-DOWN_SC_AT = 132
-Y_AT = (144, 152)
+GATE_AT = (8, 218, 24, 40, 56, 72, 88, 104)
+WORDS_AT = (8, 218)
+DOWN_AT = (24, 32)
+H_GROUPED_AT = (38, 70, 102, 234)
+UP_GROUPED_AT = (128, 234, 236, 234)
+W4_RAW_AT = 4
+W4_SC_RAW_AT = 124
+PICKED_AT = 126
+DOWN_GROUPED_AT = (196, 6)
+DOWN_CODES_AT = 136
+DOWN_SC_AT = 140
+Y_AT = (152, 0)
 V_AT = (160, 168)
 H_CODES_AT = 176
 W4_AT = 184
@@ -49,8 +49,8 @@ UP_RAW_AT = 202
 TAB_SC_AT = 216
 W4_SC_AT = 198
 H_BLOCKS_ON_VECTOR = (8, 9, 10, 13)
-STORES = ((0, 4, 112), (4, 6, 0), (6, 7, 16), (7, 8, 24))
-LAST_CUTS = (0, 1024, 1536, 2048)
+STORES = ((0, 4, 120), (4, 6, 8), (6, 7, 218), (7, 8, 226))
+LAST_CUTS = (0, 1024, 1536, 1792, 2048)
 
 
 def tile_list_tabgate_bias_kernel(
@@ -72,15 +72,14 @@ def tile_list_tabgate_bias_kernel(
             return offsets[:, j0 // LIST_ROWS : j1 // LIST_ROWS]
 
         tab_sc = placed([P, T // 4], I32, "tab_sc", TAB_SC_AT)
-        nc.vector.memset(tab_sc[:], 0)
+        nc.sync.dma_start(tab_sc[32:64, :], tab_scales.rearrange("a q t -> (a q) t").bitcast(I32))
+        nc.vector.memset(tab_sc[0:32, :], 0)
+        nc.vector.memset(tab_sc[64:P, :], 0)
         w4_sc_raw = placed([P, PASSES, M // 4], I32, "w4_sc_raw", W4_SC_RAW_AT)
         nc.vector.memset(w4_sc_raw[:], 0)
 
-        w4_raw = placed([P, PASSES, 2 * M // 4], I32, "w4_raw", W4_RAW_AT)
-        nc.sync.dma_start(w4_raw[:], w4_words.rearrange("a p c -> p a c").bitcast(I32))
         bias = placed([P, ROWS], F32, "bias", BIAS_AT)
         nc.sync.dma_start(bias[:], b.rearrange("(p u) -> p u", u=ROWS))
-        nc.sync.dma_start(tab_sc[32:96:2, :], tab_scales.rearrange("a q t -> (a q) t").bitcast(I32))
         for r in range(4):
             nc.gpsimd.dma_start(
                 w4_sc_raw[r:P:32, :, :], w4_scales[:, r:16:4, :].rearrange("a q n -> q a n").bitcast(I32)
@@ -107,8 +106,7 @@ def tile_list_tabgate_bias_kernel(
             plane = placed([P, S // 4], I32, "v_sc%d" % a, V_SC_AT[a])
             nc.vector.memset(plane[:], 0)
             for r in range(4):
-                first = 32 + 32 * a + 2 * r
-                nc.sync.dma_start(plane[r:P:32, :], picked_sc[first : first + 32 - 2 * r : 8, :].bitcast(I32))
+                nc.sync.dma_start(plane[r:P:32, :], picked_sc[32 + 16 * a + r : 48 + 16 * a : 4, :].bitcast(I32))
             v_sc.append(plane[:].bitcast(U8))
 
         place_scales(0)
@@ -118,10 +116,12 @@ def tile_list_tabgate_bias_kernel(
         nc.sync.dma_start(up_raw[:], up.rearrange("(p i) n -> p i n", i=PACK))
 
         w4 = placed([P, PASSES, ROWS, P], U16, "w4", W4_AT)
-        for u0 in range(0, ROWS, 4):
+        w4_raw = placed([P, PASSES, 2 * M // 4], I32, "w4_raw", W4_RAW_AT)
+
+        def deal_w4(u0, u1):
             nc.scalar.copy(
-                w4[:, :, u0 : u0 + 4, :].rearrange("p a u c -> p a c u"),
-                w4_raw[:].bitcast(U16).rearrange("p a (c u) -> p a c u", u=ROWS)[:, :, :, u0 : u0 + 4],
+                w4[:, :, u0:u1, :].rearrange("p a u c -> p a c u"),
+                w4_raw[:].bitcast(U16).rearrange("p a (c u) -> p a c u", u=ROWS)[:, :, :, u0:u1],
             )
 
         v_codes = [
@@ -222,21 +222,23 @@ def tile_list_tabgate_bias_kernel(
 
         for c in range(CHUNKS):
             gather_words(0, c)
-        load_gate(0)
         quantize_down(0)
         quantize_down(1)
-        load_gate(1)
+        nc.sync.dma_start(w4_raw[:], w4_words.rearrange("a p c -> p a c").bitcast(I32))
+        load_gate(0)
         w4_sc = placed([P, PASSES, ROWS, P], U8, "w4_sc", W4_SC_AT)
         nc.vector.tensor_copy(w4_sc[:], w4_sc_raw[:].bitcast(U8).rearrange("p a (c u) -> p a u c", u=ROWS))
         for c in range(CHUNKS):
             gather_words(1, c)
-        load_gate(2)
+        load_gate(1)
         make_h(0)
+        load_gate(2)
         load_gate(3)
         make_h(1)
         load_gate(4)
         load_gate(5)
         quantize_up(0)
+        deal_w4(0, 2)
         make_h(2)
         load_gate(6)
         load_gate(7)
@@ -247,6 +249,9 @@ def tile_list_tabgate_bias_kernel(
             result = placed([P, u1 - u0, S], F32, "result%d" % u0, at)
             for u in range(u0, u1):
                 y = make_y(u)
+                if u == 0:
+                    deal_w4(2, 4)
+                    deal_w4(4, ROWS)
                 if u == 0:
                     cuts = range(0, S + 1, CHUNK)
                 elif u == 1:

@@ -24,32 +24,31 @@ CHUNKS = S // CHUNK
 BLOCK = 128
 ROWS = M // P
 LIST_ROWS = 16
-UP_ROWS = 2
-GATE_AT = (8, 218, 24, 40, 56, 72, 88, 104)
-WORDS_AT = (8, 218)
-DOWN_AT = (24, 32)
-H_GROUPED_AT = (38, 70, 102, 234)
-UP_GROUPED_AT = (128, 234, 236, 234)
-W4_RAW_AT = 4
-W4_SC_RAW_AT = 124
-PICKED_AT = 126
-DOWN_GROUPED_AT = (196, 6)
-DOWN_CODES_AT = 136
-DOWN_SC_AT = 140
-Y_AT = (152, 0)
-V_AT = (160, 168)
-H_CODES_AT = 176
-W4_AT = 184
-UP_CODES_AT = 188
-V_SC_AT = (192, 194)
-H_SC_AT = 196
-UP_SC_AT = 201
-BIAS_AT = 200
-UP_RAW_AT = 202
-TAB_SC_AT = 216
-W4_SC_AT = 198
-H_BLOCKS_ON_VECTOR = (8, 9, 10, 13)
-STORES = ((0, 4, 120), (4, 6, 8), (6, 7, 218), (7, 8, 226))
+UP_PARTS = ((0, 2, 218), (2, 4, 220), (4, 8, 222))
+Y_AT = (0, 8)
+WORDS_AT = (32, 202)
+GATE_AT = (16, 202, 32, 48, 64, 80, 16, 202)
+DOWN_AT = (180, 16)
+DOWN_GROUPED_AT = (174, 24)
+H_GROUPED_AT = (46, 78, 226, 230)
+PICKED_AT = 96
+W4_SC_RAW_AT = 98
+V_AT = (128, 136)
+H_CODES_AT = 144
+W4_AT = 152
+UP_CODES_AT = 156
+V_SC_AT = (160, 162)
+H_SC_AT = 164
+UP_SC_AT = 166
+BIAS_AT = 167
+DOWN_CODES_AT = 168
+DOWN_SC_AT = 172
+W4_SC_AT = 174
+UP_RAW_AT = 180
+W4_RAW_AT = 196
+TAB_SC_AT = 199
+H_BLOCKS_ON_VECTOR = (8, 9, 12)
+STORES = ((0, 4, 96), (4, 6, 32), (6, 7, 48), (7, 8, 56))
 LAST_CUTS = (0, 1024, 1536, 1792, 2048)
 
 
@@ -112,11 +111,10 @@ def tile_list_tabgate_bias_kernel(
         place_scales(0)
         words.append(load_words(1))
         place_scales(1)
-        up_raw = placed([P, PACK, M], F32, "up_raw", UP_RAW_AT)
-        nc.sync.dma_start(up_raw[:], up.rearrange("(p i) n -> p i n", i=PACK))
 
         w4 = placed([P, PASSES, ROWS, P], U16, "w4", W4_AT)
         w4_raw = placed([P, PASSES, 2 * M // 4], I32, "w4_raw", W4_RAW_AT)
+        nc.sync.dma_start(w4_raw[:], w4_words.rearrange("a p c -> p a c").bitcast(I32))
 
         def deal_w4(u0, u1):
             nc.scalar.copy(
@@ -124,9 +122,10 @@ def tile_list_tabgate_bias_kernel(
                 w4_raw[:].bitcast(U16).rearrange("p a (c u) -> p a c u", u=ROWS)[:, :, :, u0:u1],
             )
 
+        v_first = placed([P, S], U32, "v_codes0", V_AT[0])
         v_codes = [
-            [placed([P, CHUNK], U32, "v_codes%d_%d" % (a, c), V_AT[a] + 2 * c) for c in range(CHUNKS)]
-            for a in range(PASSES)
+            [v_first[:, c * CHUNK : (c + 1) * CHUNK] for c in range(CHUNKS)],
+            [placed([P, CHUNK], U32, "v_codes1_%d" % c, V_AT[1] + 2 * c)[:] for c in range(CHUNKS)],
         ]
         down_codes = placed([P, PASSES, R], U32, "down_codes", DOWN_CODES_AT)
         down_sc = placed([P, PASSES, R], U8, "down_sc", DOWN_SC_AT)
@@ -137,7 +136,7 @@ def tile_list_tabgate_bias_kernel(
 
         def gather_words(a, c):
             nc.vector.tensor_copy(
-                v_codes[a][c][:], words[a][:].bitcast(U32).indirect(entries(c * CHUNK, (c + 1) * CHUNK))
+                v_codes[a][c], words[a][:].bitcast(U32).indirect(entries(c * CHUNK, (c + 1) * CHUNK))
             )
 
         def quantize_down(a):
@@ -149,12 +148,12 @@ def tile_list_tabgate_bias_kernel(
             nc.vector.quantize_mx(down_codes[:, a, :].bitcast(FP8X4), down_sc[:, a, :], grouped[:])
 
         def quantize_up(part):
-            u0 = part * UP_ROWS
-            cols = slice(u0 * P, (u0 + UP_ROWS) * P)
-            grouped = placed([P, PACK * UP_ROWS * P], BF16, "up_grouped%d" % part, UP_GROUPED_AT[part])
+            u0, u1, at = UP_PARTS[part]
+            cols = slice(u0 * P, u1 * P)
+            grouped = placed([P, PACK * (u1 - u0) * P], BF16, "up_grouped%d" % part, at)
             nc.scalar.copy(
-                grouped[:].rearrange("p (u c i) -> p c u i", u=UP_ROWS, i=PACK),
-                up_raw[:].rearrange("p i (c u) -> p c u i", u=ROWS)[:, :, u0 : u0 + UP_ROWS, :],
+                grouped[:].rearrange("p (u c i) -> p c u i", u=u1 - u0, i=PACK),
+                up_raw[:].rearrange("p i (c u) -> p c u i", u=ROWS)[:, :, u0:u1, :],
             )
             nc.vector.quantize_mx(up_codes[:, cols].bitcast(FP8X4), up_sc[:, cols], grouped[:])
 
@@ -200,7 +199,7 @@ def tile_list_tabgate_bias_kernel(
                         bank[:],
                         lhsT=w4[:, a, u, :].bitcast(U8).bitcast(FP4X4),
                         lhsT_scale=w4_sc[:, a, u, :],
-                        rhs=v_codes[a][c][:].bitcast(FP8X4),
+                        rhs=v_codes[a][c].bitcast(FP8X4),
                         rhs_scale=v_sc[a][:, cols],
                         start=(a == 0),
                         stop=False,
@@ -220,17 +219,18 @@ def tile_list_tabgate_bias_kernel(
         def gate_cols(u, y, result, j0, j1):
             nc.vector.tensor_tensor(result[:, j0:j1], gates[u][:].indirect(entries(j0, j1)), y[:, j0:j1], MULT)
 
-        for c in range(CHUNKS):
-            gather_words(0, c)
+        nc.vector.tensor_copy(v_first[:], words[0][:].bitcast(U32).indirect(offsets[:]))
         quantize_down(0)
+        up_raw = placed([P, PACK, M], F32, "up_raw", UP_RAW_AT)
+        nc.sync.dma_start(up_raw[:], up.rearrange("(p i) n -> p i n", i=PACK))
         quantize_down(1)
-        nc.sync.dma_start(w4_raw[:], w4_words.rearrange("a p c -> p a c").bitcast(I32))
         load_gate(0)
         w4_sc = placed([P, PASSES, ROWS, P], U8, "w4_sc", W4_SC_AT)
         nc.vector.tensor_copy(w4_sc[:], w4_sc_raw[:].bitcast(U8).rearrange("p a (c u) -> p a u c", u=ROWS))
         for c in range(CHUNKS):
             gather_words(1, c)
         load_gate(1)
+        deal_w4(0, 2)
         make_h(0)
         load_gate(2)
         load_gate(3)
@@ -238,10 +238,7 @@ def tile_list_tabgate_bias_kernel(
         load_gate(4)
         load_gate(5)
         quantize_up(0)
-        deal_w4(0, 2)
         make_h(2)
-        load_gate(6)
-        load_gate(7)
         make_h(3)
 
         out_rows = out.rearrange("(p u) j -> p u j", u=ROWS)
@@ -251,6 +248,7 @@ def tile_list_tabgate_bias_kernel(
                 y = make_y(u)
                 if u == 0:
                     deal_w4(2, 4)
+                if u == 1:
                     deal_w4(4, ROWS)
                 if u == 0:
                     cuts = range(0, S + 1, CHUNK)
@@ -264,7 +262,8 @@ def tile_list_tabgate_bias_kernel(
                     gate_cols(u, y, result[:, u - u0, :], j0, j1)
                     if u == ROWS - 1:
                         nc.sync.dma_start(out_rows[:, u, j0:j1], result[:, u - u0, j0:j1])
-                if u + 1 < ROWS // UP_ROWS:
+                if u < 2:
+                    load_gate(ROWS - 2 + u)
                     quantize_up(u + 1)
             if u1 < ROWS:
                 nc.sync.dma_start(out_rows[:, u0:u1, :], result[:])

@@ -250,9 +250,9 @@ def tile_list_tabgate_bias_kernel(
                     deal_w4(2, 4)
                 if u == 1:
                     deal_w4(4, ROWS)
-                if u == 0:
+                if u < 2:
                     cuts = range(0, S + 1, CHUNK)
-                elif u == 1:
+                elif u < 4:
                     cuts = range(0, S + 1, S // 2)
                 elif u == ROWS - 1:
                     cuts = LAST_CUTS

from contextlib import ExitStack

import concourse.mybir as mybir

K, M, T, S, R = 1024, 1024, 4096, 2048, 512
FLOPS = 2 * S * (K * M + K * R + R * M)

F32 = mybir.dt.float32
BF16 = mybir.dt.bfloat16
I32 = mybir.dt.int32
U32 = mybir.dt.uint32
U16 = mybir.dt.uint16
U8 = mybir.dt.uint8
FP8X4 = mybir.dt.float8_e4m3fn_x4
FP4X4 = mybir.dt.float4_e2m1fn_x4
MULT = mybir.AluOpType.mult
IDENTITY = mybir.ActivationFunctionType.Identity

P = 128
PACK = 4
PASSES = K // (P * PACK)
CHUNK = 512
CHUNKS = S // CHUNK
BLOCK = 128
ROWS = M // P
LIST_ROWS = 16
UP_PARTS = ((0, 2, 218), (2, 4, 220), (4, 8, 222))
Y_AT = (0, 8)
WORDS_AT = (32, 202)
GATE_AT = (16, 202, 32, 48, 64, 80, 16, 202)
DOWN_AT = (180, 16)
DOWN_GROUPED_AT = (174, 24)
H_GROUPED_AT = (46, 78, 226, 230)
PICKED_AT = 96
W4_SC_RAW_AT = 98
V_AT = (128, 136)
H_CODES_AT = 144
W4_AT = 152
UP_CODES_AT = 156
V_SC_AT = (160, 162)
H_SC_AT = 164
UP_SC_AT = 166
BIAS_AT = 167
DOWN_CODES_AT = 168
DOWN_SC_AT = 172
W4_SC_AT = 174
UP_RAW_AT = 180
W4_RAW_AT = 196
TAB_SC_AT = 199
H_BLOCKS_ON_VECTOR = (8, 9, 12)
STORES = ((0, 4, 96), (4, 6, 32), (6, 7, 48), (7, 8, 56))
LAST_CUTS = (0, 1024, 1536, 1792, 2048)


def tile_list_tabgate_bias_kernel(
    tc, tab_words, tab_scales, w4_words, w4_scales, down, up, gT, b, offs, out
):
    nc = tc.nc
    with ExitStack() as ctx:
        keep = ctx.enter_context(tc.tile_pool(name="keep", bufs=1))
        space = ctx.enter_context(tc.tile_pool(name="space", bufs=1))
        psum = ctx.enter_context(tc.psum_pool(name="psum", bufs=8))

        def placed(shape, dtype, name, kib):
            return space.tile(shape, dtype, name=name, offset=kib * 1024, align_bytes=256)

        offsets = keep.tile([P, S // LIST_ROWS], U16, name="offsets")
        nc.sync.dma_start(offsets[:], offs)

        def entries(j0, j1):
            return offsets[:, j0 // LIST_ROWS : j1 // LIST_ROWS]

        tab_sc = placed([P, T // 4], I32, "tab_sc", TAB_SC_AT)
        nc.sync.dma_start(tab_sc[32:64, :], tab_scales.rearrange("a q t -> (a q) t").bitcast(I32))
        nc.vector.memset(tab_sc[0:32, :], 0)
        nc.vector.memset(tab_sc[64:P, :], 0)
        w4_sc_raw = placed([P, PASSES, M // 4], I32, "w4_sc_raw", W4_SC_RAW_AT)
        nc.vector.memset(w4_sc_raw[:], 0)

        bias = placed([P, ROWS], F32, "bias", BIAS_AT)
        nc.sync.dma_start(bias[:], b.rearrange("(p u) -> p u", u=ROWS))
        for r in range(4):
            nc.gpsimd.dma_start(
                w4_sc_raw[r:P:32, :, :], w4_scales[:, r:16:4, :].rearrange("a q n -> q a n").bitcast(I32)
            )

        def load_words(a):
            window = placed([P, T], I32, "window%d" % a, WORDS_AT[a])
            nc.sync.dma_start(window[:], tab_words[a].rearrange("p t i -> p (t i)").bitcast(I32))
            return window

        def load_down(a):
            raw = placed([P, PACK, R], F32, "down_raw%d" % a, DOWN_AT[a])
            nc.sync.dma_start(raw[:], down.rearrange("(a p i) r -> a p i r", p=P, i=PACK)[a])
            return raw

        words = [load_words(0)]
        down_raw = [load_down(a) for a in range(PASSES)]

        picked_sc = placed([P, S], U8, "picked_sc", PICKED_AT)
        nc.vector.tensor_copy(picked_sc[:], tab_sc[:].bitcast(U8).indirect(offsets[:]))
        v_sc = []

        def place_scales(a):
            plane = placed([P, S // 4], I32, "v_sc%d" % a, V_SC_AT[a])
            nc.vector.memset(plane[:], 0)
            for r in range(4):
                nc.sync.dma_start(plane[r:P:32, :], picked_sc[32 + 16 * a + r : 48 + 16 * a : 4, :].bitcast(I32))
            v_sc.append(plane[:].bitcast(U8))

        place_scales(0)
        words.append(load_words(1))
        place_scales(1)

        w4 = placed([P, PASSES, ROWS, P], U16, "w4", W4_AT)
        w4_raw = placed([P, PASSES, 2 * M // 4], I32, "w4_raw", W4_RAW_AT)
        nc.sync.dma_start(w4_raw[:], w4_words.rearrange("a p c -> p a c").bitcast(I32))

        def deal_w4(u0, u1):
            nc.scalar.copy(
                w4[:, :, u0:u1, :].rearrange("p a u c -> p a c u"),
                w4_raw[:].bitcast(U16).rearrange("p a (c u) -> p a c u", u=ROWS)[:, :, :, u0:u1],
            )

        v_first = placed([P, S], U32, "v_codes0", V_AT[0])
        v_codes = [
            [v_first[:, c * CHUNK : (c + 1) * CHUNK] for c in range(CHUNKS)],
            [placed([P, CHUNK], U32, "v_codes1_%d" % c, V_AT[1] + 2 * c)[:] for c in range(CHUNKS)],
        ]
        down_codes = placed([P, PASSES, R], U32, "down_codes", DOWN_CODES_AT)
        down_sc = placed([P, PASSES, R], U8, "down_sc", DOWN_SC_AT)
        up_codes = placed([P, M], U32, "up_codes", UP_CODES_AT)
        up_sc = placed([P, M], U8, "up_sc", UP_SC_AT)
        h_codes = placed([P, S], U32, "h_codes", H_CODES_AT)
        h_sc = placed([P, S], U8, "h_sc", H_SC_AT)

        def gather_words(a, c):
            nc.vector.tensor_copy(
                v_codes[a][c], words[a][:].bitcast(U32).indirect(entries(c * CHUNK, (c + 1) * CHUNK))
            )

        def quantize_down(a):
            grouped = placed([P, PACK * R], BF16, "down_grouped%d" % a, DOWN_GROUPED_AT[a])
            nc.scalar.copy(
                grouped[:].rearrange("p (t m i) -> p m i t", t=PACK, i=PACK),
                down_raw[a][:].rearrange("p i (m t) -> p m i t", t=PACK),
            )
            nc.vector.quantize_mx(down_codes[:, a, :].bitcast(FP8X4), down_sc[:, a, :], grouped[:])

        def quantize_up(part):
            u0, u1, at = UP_PARTS[part]
            cols = slice(u0 * P, u1 * P)
            grouped = placed([P, PACK * (u1 - u0) * P], BF16, "up_grouped%d" % part, at)
            nc.scalar.copy(
                grouped[:].rearrange("p (u c i) -> p c u i", u=u1 - u0, i=PACK),
                up_raw[:].rearrange("p i (c u) -> p c u i", u=ROWS)[:, :, u0:u1, :],
            )
            nc.vector.quantize_mx(up_codes[:, cols].bitcast(FP8X4), up_sc[:, cols], grouped[:])

        def make_h(c):
            grouped = placed([P, PACK * CHUNK], BF16, "h_grouped%d" % c, H_GROUPED_AT[c])
            for blk in range(CHUNK // BLOCK):
                j0 = c * CHUNK + blk * BLOCK
                cols = slice(blk * BLOCK, (blk + 1) * BLOCK)
                bank = psum.tile([P, PACK, BLOCK], F32, name="h_bank", tag="bank")
                for a in range(PASSES):
                    for t in range(PACK):
                        nc.tensor.matmul_mx(
                            bank[:, t, :],
                            lhsT=down_codes[:, a, t * P : (t + 1) * P].bitcast(FP8X4),
                            lhsT_scale=down_sc[:, a, t * P : (t + 1) * P],
                            rhs=v_codes[a][c][:, cols].bitcast(FP8X4),
                            rhs_scale=v_sc[a][:, j0 : j0 + BLOCK],
                            start=(a == 0 and t == 0),
                            stop=(a == PASSES - 1 and t == PACK - 1),
                        )
                copy = nc.vector.tensor_copy if j0 // BLOCK in H_BLOCKS_ON_VECTOR else nc.scalar.copy
                copy(
                    grouped[:, PACK * BLOCK * blk : PACK * BLOCK * (blk + 1)].rearrange("p (n t) -> p n t", t=PACK),
                    bank[:].rearrange("p t n -> p n t"),
                )
            cols = slice(c * CHUNK, (c + 1) * CHUNK)
            nc.vector.quantize_mx(h_codes[:, cols].bitcast(FP8X4), h_sc[:, cols], grouped[:])

        gates = []

        def load_gate(u):
            gate = placed([P, T], F32, "gate%d" % u, GATE_AT[u])
            nc.sync.dma_start(gate[:], gT.rearrange("(p u) t -> u p t", u=ROWS)[u])
            gates.append(gate)

        def make_y(u):
            y = placed([P, S], F32, "y%d" % u, Y_AT[u % 2])
            for c in range(CHUNKS):
                cols = slice(c * CHUNK, (c + 1) * CHUNK)
                bank = psum.tile([P, CHUNK], F32, name="y_bank", tag="bank")
                for a in range(PASSES):
                    nc.tensor.matmul_mx(
                        bank[:],
                        lhsT=w4[:, a, u, :].bitcast(U8).bitcast(FP4X4),
                        lhsT_scale=w4_sc[:, a, u, :],
                        rhs=v_codes[a][c].bitcast(FP8X4),
                        rhs_scale=v_sc[a][:, cols],
                        start=(a == 0),
                        stop=False,
                    )
                nc.tensor.matmul_mx(
                    bank[:],
                    lhsT=up_codes[:, u * P : (u + 1) * P].bitcast(FP8X4),
                    lhsT_scale=up_sc[:, u * P : (u + 1) * P],
                    rhs=h_codes[:, cols].bitcast(FP8X4),
                    rhs_scale=h_sc[:, cols],
                    start=False,
                    stop=True,
                )
                nc.scalar.activation(y[:, cols], bank[:], IDENTITY, bias=bias[:, u : u + 1])
            return y

        def gate_cols(u, y, result, j0, j1):
            nc.vector.tensor_tensor(result[:, j0:j1], gates[u][:].indirect(entries(j0, j1)), y[:, j0:j1], MULT)

        nc.vector.tensor_copy(v_first[:], words[0][:].bitcast(U32).indirect(offsets[:]))
        quantize_down(0)
        up_raw = placed([P, PACK, M], F32, "up_raw", UP_RAW_AT)
        nc.sync.dma_start(up_raw[:], up.rearrange("(p i) n -> p i n", i=PACK))
        quantize_down(1)
        load_gate(0)
        w4_sc = placed([P, PASSES, ROWS, P], U8, "w4_sc", W4_SC_AT)
        nc.vector.tensor_copy(w4_sc[:], w4_sc_raw[:].bitcast(U8).rearrange("p a (c u) -> p a u c", u=ROWS))
        for c in range(CHUNKS):
            gather_words(1, c)
        load_gate(1)
        deal_w4(0, 2)
        make_h(0)
        load_gate(2)
        load_gate(3)
        make_h(1)
        load_gate(4)
        load_gate(5)
        quantize_up(0)
        make_h(2)
        make_h(3)

        out_rows = out.rearrange("(p u) j -> p u j", u=ROWS)
        for u0, u1, at in STORES:
            result = placed([P, u1 - u0, S], F32, "result%d" % u0, at)
            for u in range(u0, u1):
                y = make_y(u)
                if u == 0:
                    deal_w4(2, 4)
                if u == 1:
                    deal_w4(4, ROWS)
                if u < 2:
                    cuts = range(0, S + 1, CHUNK)
                elif u < 4:
                    cuts = range(0, S + 1, S // 2)
                elif u == ROWS - 1:
                    cuts = LAST_CUTS
                else:
                    cuts = (0, S)
                for j0, j1 in zip(cuts, cuts[1:]):
                    gate_cols(u, y, result[:, u - u0, :], j0, j1)
                    if u == ROWS - 1:
                        nc.sync.dma_start(out_rows[:, u, j0:j1], result[:, u - u0, j0:j1])
                if u < 2:
                    load_gate(ROWS - 2 + u)
                    quantize_up(u + 1)
            if u1 < ROWS:
                nc.sync.dma_start(out_rows[:, u0:u1, :], result[:])
